import numpy as np
import ml_dtypes


def mxq(x, axis, fmt="e4m3"):
    dtype, down = {"e4m3": (ml_dtypes.float8_e4m3fn, 7), "e5m2": (ml_dtypes.float8_e5m2, 14)}[fmt]
    v = np.moveaxis(np.asarray(x, np.float32).astype(ml_dtypes.bfloat16).astype(np.float64), axis, -1)
    blocks = v.reshape(v.shape[:-1] + (-1, 32))
    amax = np.abs(blocks).max(-1, keepdims=True)
    byte = np.maximum(np.where(amax > 0, np.frexp(amax)[1] - 1 + 127, 0) - down, 1)
    scale = np.exp2(byte - 127.0)
    codes = (blocks / scale).astype(np.float32).astype(dtype).astype(np.float64)
    return np.moveaxis((codes * scale).reshape(v.shape), -1, axis)


WIDE = False


def mx_kscale(k):
    if not WIDE:
        return np.ones(k)
    levels = np.array([10, -10, 5, -5, 0])
    if k % 512:
        return np.exp2(np.random.permutation(np.resize(levels, k // 32))).repeat(32)
    a = np.empty((k // 512, 16))
    for p in range(k // 512):
        a[p, :8] = np.random.permutation(np.resize(levels, 8))
        for g in range(8):
            far = levels[np.abs(levels - a[p, g]) >= 10]
            a[p, g + 8] = far[np.random.randint(len(far))]
    return np.exp2(a.ravel()).repeat(32)


def f64(x):
    return np.asarray(x).astype(np.float64)


def striped(idx):
    return np.tile(idx.reshape(-1, 16).T, (8, 1)).astype(np.uint16)


def unstriped(offs):
    return offs[:16].T.reshape(-1).astype(np.int64)


def striped8(idx):
    return np.concatenate([x.reshape(-1, 16).T for x in idx]).astype(np.uint16)


def runs(offs, k):
    lists = np.stack([offs[16 * r : 16 * r + 16].T.reshape(-1) for r in range(8)]).astype(np.int64)
    return lists[np.arange(k) % 512 // 64]


def pack_weight(w):
    k, n = w.shape
    w = f64(np.asarray(w, np.float32).astype(ml_dtypes.bfloat16)).reshape(k // 32, 32, n)
    amax = np.abs(w).max(1)
    byte = np.clip(np.where(amax > 0, np.frexp(amax)[1] - 1 + 127 - 7, 1), 1, 254)
    scaled = (w * np.exp2(127.0 - byte)[:, None, :]).reshape(k, n).astype(np.float32)
    words = np.ascontiguousarray(scaled.reshape(k // 512, 128, 4, n).transpose(0, 1, 3, 2)).astype(ml_dtypes.float8_e4m3fn).view(np.uint8)
    return words, np.ascontiguousarray(byte.astype(np.uint8).reshape(k // 512, 16, n))


def unpack_weight(words, scales):
    g, p, n, _ = words.shape
    vals = np.ascontiguousarray(words).view(ml_dtypes.float8_e4m3fn).astype(np.float64) * np.repeat(np.exp2(scales.astype(np.float64) - 127.0), 8, axis=1)[..., None]
    return vals.transpose(0, 1, 3, 2).reshape(g * 512, n)


E2M1 = np.array([0.0, 0.5, 1.0, 1.5, 2.0, 3.0, 4.0, 6.0, -0.0, -0.5, -1.0, -1.5, -2.0, -3.0, -4.0, -6.0])


def pack_fp4(w):
    k, n = w.shape
    w = f64(np.asarray(w, np.float32).astype(ml_dtypes.bfloat16)).reshape(k // 32, 32, n)
    amax = np.abs(w).max(1)
    mant, ex = np.frexp(amax / 6.0)
    byte = np.clip(np.where(amax > 0, np.where(mant > 0.5, ex, ex - 1) + 127, 1), 1, 254)
    scaled = (w * np.exp2(127.0 - byte)[:, None, :]).reshape(k, n).astype(np.float32)
    c = np.ascontiguousarray(scaled.reshape(k // 512, 128, 4, n).transpose(0, 1, 3, 2)).astype(ml_dtypes.float4_e2m1fn).view(np.uint8) & 0xF
    words = (c[..., 0::2] | (c[..., 1::2] << 4)).reshape(k // 512, 128, 2 * n)
    return np.ascontiguousarray(words), np.ascontiguousarray(byte.astype(np.uint8).reshape(k // 512, 16, n))


def unpack_fp4(words, scales):
    g, _, n = scales.shape
    words = np.ascontiguousarray(words).reshape(g, 128, n, 2)
    nib = np.empty((g, 128, n, 4), np.uint8)
    nib[..., 0::2] = words & 0xF
    nib[..., 1::2] = words >> 4
    vals = E2M1[nib] * np.repeat(np.exp2(scales.astype(np.float64) - 127.0), 8, axis=1)[..., None]
    return vals.transpose(0, 1, 3, 2).reshape(g * 512, n)


def relu(v):
    return np.maximum(v, 0.0)

def planes(y):
    n, m = y.shape
    v = y.astype(np.float32).astype(ml_dtypes.bfloat16).astype(np.float64).reshape(n // 32, 32, m)
    top = np.abs(v).max(1)
    byte = np.clip(np.where(top > 0, np.frexp(top)[1] - 1 + 127 - 7, 1), 1, 254)
    codes = (v * np.exp2(127.0 - byte)[:, None, :]).reshape(n, m).astype(np.float32).astype(ml_dtypes.float8_e4m3fn).view(np.uint8)
    words = codes.reshape(n // 512, 128, 4, m).transpose(0, 1, 3, 2)
    return np.ascontiguousarray(words), np.ascontiguousarray(byte.astype(np.uint8).reshape(n // 512, 16, m))


K, T, S, N, G, H = 512, 2048, 512, 512, 2048, 512


def setup_inputs():
    n = np.random.standard_normal
    s = mx_kscale(K)[:, None]
    u = mx_kscale(H)
    packed_xT = pack_weight(n((K, T)) * s)
    packed_dT = pack_weight(n((K, G)) / s)
    packed_w1 = pack_fp4(n((H, N)) / np.sqrt(H) / u[:, None])
    return {
        "x_words": packed_xT[0],
        "x_scales": packed_xT[1],
        "d_words": packed_dT[0],
        "d_scales": packed_dT[1],
        "gn": (np.random.uniform(0.5, 1.5, (H, 1)) * u[:, None]).astype(np.float32),
        "w1_words": packed_w1[0],
        "w1_scales": packed_w1[1],
        "offs": striped(np.random.permutation(T)[:S]),
        "k1": striped8(np.random.randint(0, G, (8, H))),
        "k2": striped8(np.random.randint(0, G, (8, H))),
    }


def reference(x_words, x_scales, d_words, d_scales, gn, w1_words, w1_scales, offs, k1, k2):
    d_k1 = unpack_weight(d_words, d_scales)[np.arange(K)[:, None], runs(k1, K)]
    xq = unpack_weight(x_words, x_scales)[:, unstriped(offs)]
    d_k2 = unpack_weight(d_words, d_scales)[np.arange(K)[:, None], runs(k2, K)]
    s = 0.0625 * ((d_k1.T @ xq) + 0.5 * (d_k2.T @ xq))
    z = f64(gn) * relu(s)
    out_0 = unpack_fp4(w1_words, w1_scales).T @ mxq(z, 0, "e4m3")
    return (out_0,) + planes(out_0)

@@ -1,0 +1,191 @@
+from contextlib import ExitStack
+
+import concourse.mybir as mybir
+from concourse.masks import make_identity
+
+K, T, S, N, G, H = 512, 2048, 512, 512, 2048, 512
+FLOPS = 2 * K * H * S * 2 + 2 * H * N * S
+
+F32 = mybir.dt.float32
+BF16 = mybir.dt.bfloat16
+I32 = mybir.dt.int32
+U32 = mybir.dt.uint32
+U16 = mybir.dt.uint16
+U8 = mybir.dt.uint8
+FP8X4 = mybir.dt.float8_e4m3fn_x4
+FP4X4 = mybir.dt.float4_e2m1fn_x4
+ALU = mybir.AluOpType
+ACT = mybir.ActivationFunctionType
+
+P = 128
+TILES = S // P
+HALF = S // 2
+
+
+def tile_picked_rpqscore_relu_po_kernel(
+    tc, x_words, x_scales, d_words, d_scales, gn, w1_words, w1_scales, offs, k1, k2, out_0, out_1, out_2
+):
+    nc = tc.nc
+    with ExitStack() as ctx:
+        keep = ctx.enter_context(tc.tile_pool(name="keep", bufs=1))
+        psum = ctx.enter_context(tc.psum_pool(name="psum", bufs=1))
+
+        offs_t = keep.tile([P, S // 16], U16, name="offs_t")
+        k1_t = keep.tile([P, H // 16], U16, name="k1_t")
+        k2_t = keep.tile([P, H // 16], U16, name="k2_t")
+        x_table = keep.tile([P, T], I32, name="x_table", align_bytes=64)
+        d_table = keep.tile([P, G], I32, name="d_table", align_bytes=64)
+        xs_table = keep.tile([P, T], U8, name="xs_table", align_bytes=64)
+        ds_table = keep.tile([P, G], U8, name="ds_table", align_bytes=64)
+        picked_scales = keep.tile([P, 2 * H + S], U8, name="picked_scales", align_bytes=64)
+        planes = keep.tile([P, 2 * H + S], U8, name="planes", align_bytes=64)
+        w_raw = keep.tile([P, 2 * N], U8, name="w_raw", align_bytes=64)
+        w_dealt = keep.tile([P, 2 * N], U8, name="w_dealt", align_bytes=64)
+        ws_raw = keep.tile([P, N], U8, name="ws_raw", align_bytes=64)
+        ws_dealt = keep.tile([P, N], U8, name="ws_dealt", align_bytes=64)
+        g_cols = keep.tile([P, 4], F32, name="g_cols")
+        g_rows = keep.tile([P, 2, P, 2], F32, name="g_rows", align_bytes=64)
+        ident = keep.tile([P, P], F32, name="ident")
+
+        nc.vector.memset(xs_table[:].bitcast(I32), 0)
+        nc.vector.memset(planes[:].bitcast(I32), 0)
+        nc.vector.memset(ws_raw[:].bitcast(I32), 0)
+        make_identity(nc, ident[:])
+
+        nc.sync.dma_start(k2_t[:], k2)
+        nc.sync.dma_start(ds_table[:].bitcast(I32), d_scales[0].bitcast(I32).unsqueeze(1).to_broadcast([16, 8, G // 4]))
+        nc.sync.dma_start(xs_table[0:P:8, :].bitcast(I32), x_scales[0].bitcast(I32))
+        nc.sync.dma_start(k1_t[:], k1)
+        nc.sync.dma_start(offs_t[:], offs)
+        nc.sync.dma_start(g_cols[:], gn.rearrange("(p t) o -> p (t o)", t=4))
+        nc.sync.dma_start(x_table[:], x_words[0].rearrange("p n t -> p (n t)").bitcast(I32))
+        nc.sync.dma_start(d_table[:], d_words[0].rearrange("p n t -> p (n t)").bitcast(I32))
+        nc.sync.dma_start(w_raw[:].bitcast(I32), w1_words[0].bitcast(I32))
+        for q in range(4):
+            nc.gpsimd.dma_start(ws_raw[32 * q : 32 * q + 4, :].bitcast(I32), w1_scales[0, 4 * q : 4 * q + 4, :].bitcast(I32))
+
+        g_bank = psum.tile([P, 4, P], F32, name="g_bank", tag="out_bank", bufs=2)
+        for t in range(4):
+            nc.tensor.transpose(g_bank[:, t, :], g_cols[:, t : t + 1].to_broadcast([P, P]), ident[:])
+        nc.scalar.activation(g_rows[:], g_bank[:].rearrange("p (u e) m -> p u m e", e=2), ACT.Copy, scale=0.03125)
+
+        nc.vector.tensor_copy(picked_scales[:, 0:H], ds_table[:].indirect(k2_t[:]))
+        nc.vector.tensor_copy(picked_scales[:, H : 2 * H], ds_table[:].indirect(k1_t[:]))
+        nc.vector.tensor_copy(picked_scales[:, 2 * H :], xs_table[:].indirect(offs_t[:]))
+        for q in range(4):
+            nc.scalar.dma_start(
+                planes[32 * q : 32 * q + 4, :].bitcast(I32), picked_scales[32 * q : 32 * q + 32 : 8, :].bitcast(I32)
+            )
+        d2_scale = planes[:, 0:H]
+        d1_scale = planes[:, H : 2 * H]
+
+        nc.gpsimd.tensor_copy(
+            w_dealt[:].rearrange("p (t m b) -> p t m b", t=4, b=2), w_raw[:].rearrange("p (m t b) -> p t m b", t=4, b=2)
+        )
+        nc.gpsimd.tensor_copy(ws_dealt[:].rearrange("p (t m) -> p t m", t=4), ws_raw[:].rearrange("p (m t) -> p t m", t=4))
+
+        d2 = keep.tile([P, H], U32, name="d2", align_bytes=64)
+        d1 = keep.tile([P, H], U32, name="d1", align_bytes=64)
+        xq = keep.tile([P, S], U32, name="xq", align_bytes=64)
+        nc.vector.tensor_copy(xq[:], x_table[:].bitcast(U32).indirect(offs_t[:]))
+        nc.vector.tensor_copy(d2[:], d_table[:].bitcast(U32).indirect(k2_t[:]))
+        nc.vector.tensor_copy(d1[:], d_table[:].bitcast(U32).indirect(k1_t[:]))
+
+        def score_pass(bank, c, keys, key_scale, start, stop):
+            nc.tensor.matmul_mx(
+                out=bank[:],
+                lhsT=xq[:, P * c : P * (c + 1)].bitcast(FP8X4),
+                lhsT_scale=planes[:, 2 * H + P * c : 2 * H + P * (c + 1)],
+                rhs=keys[:].bitcast(FP8X4),
+                rhs_scale=key_scale,
+                start=start,
+                stop=stop,
+            )
+
+        fine_bank = psum.tile([P, H], F32, name="fine_bank", tag="out_bank", bufs=2)
+        score_pass(fine_bank, 0, d2, d2_scale, True, True)
+        fine = keep.tile([P, H], F32, name="fine")
+        nc.scalar.copy(fine[:], fine_bank[:])
+        banks = [psum.tile([P, H], F32, name=f"score{c}", tag=f"score{c}") for c in range(TILES)]
+        score_pass(banks[1], 1, d2, d2_scale, True, False)
+        summed = keep.tile([P, H], F32, name="summed")
+        scores = [summed] + banks[1:]
+
+        y_codes = keep.tile([P, S], I32, name="y_codes", align_bytes=64)
+        y_scales = keep.tile([P, S], U8, name="y_scales", align_bytes=64)
+        out_rows = out_0.rearrange("(p t) j -> p t j", t=4)
+        out_words = out_1[0].rearrange("p j t -> p (j t)").bitcast(I32)
+
+        z_rows = [keep.tile([P, 2, P, 2], BF16, name=f"z_rows{c}", align_bytes=64) for c in range(TILES)]
+        z_cols = [keep.tile([P, P, 4], BF16, name=f"z_cols{c}", align_bytes=64) for c in range(TILES)]
+        z_codes = [keep.tile([P, P], U32, name=f"z_codes{c}", align_bytes=64) for c in range(TILES)]
+        z_scales = [keep.tile([P, P], U8, name=f"z_scales{c}", align_bytes=64) for c in range(TILES)]
+        y = [keep.tile([P, 4, P], F32, name=f"y{c}", align_bytes=64) for c in range(TILES)]
+        y_round = [keep.tile([P, P, 4], BF16, name=f"y_round{c}", align_bytes=64) for c in range(TILES)]
+
+        def score(c):
+            if c == 0:
+                score_pass(banks[0], 0, d1, d1_scale, True, True)
+                nc.vector.scalar_tensor_tensor(summed[:], banks[0][:], 2.0, fine[:], ALU.mult, ALU.add)
+            else:
+                if c > 1:
+                    score_pass(banks[c], c, d2, d2_scale, True, False)
+                score_pass(banks[c], c, d1, d1_scale, False, False)
+                score_pass(banks[c], c, d1, d1_scale, False, True)
+
+        def weigh(c):
+            view = scores[c][:].rearrange("p (m u e) -> p u m e", u=2, e=2)
+            for u in range(2):
+                nc.vector.scalar_tensor_tensor(z_rows[c][:, u], view[:, u], 0.0, g_rows[:, u], ALU.max, ALU.mult)
+
+        def turn(c):
+            turned = psum.tile([P, 2, P], F32, name="turned", tag="turned", bufs=2)
+            words = z_rows[c][:].rearrange("p u m e -> p (u m e)").bitcast(F32)
+            for u in range(2):
+                nc.tensor.transpose(turned[:, u, :], words[:, P * u : P * (u + 1)], ident[:])
+            nc.scalar.copy(
+                z_cols[c][:].rearrange("p j t -> p (j t)").bitcast(F32).rearrange("p (j u) -> p j u", u=2),
+                turned[:].rearrange("p u j -> p j u"),
+            )
+
+        def quantise_z(c):
+            nc.vector.quantize_mx(
+                out=z_codes[c][:].bitcast(FP8X4), scales=z_scales[c][:], in_=z_cols[c][:].rearrange("p j t -> p (j t)")
+            )
+
+        def values(c):
+            bank = psum.tile([P, 4, P], F32, name="out_bank", tag="out_bank", bufs=2)
+            for t in range(4):
+                nc.tensor.matmul_mx(
+                    out=bank[:, t, :],
+                    lhsT=w_dealt[:, 2 * P * t : 2 * P * (t + 1)].bitcast(FP4X4),
+                    lhsT_scale=ws_dealt[:, P * t : P * (t + 1)],
+                    rhs=z_codes[c][:].bitcast(FP8X4),
+                    rhs_scale=z_scales[c][:],
+                    start=True,
+                    stop=True,
+                )
+            nc.scalar.copy(y[c][:], bank[:])
+            nc.sync.dma_start(out_rows[:, :, P * c : P * (c + 1)], y[c][:])
+
+        def round_y(c):
+            nc.vector.tensor_copy(y_round[c][:], y[c][:].rearrange("p t j -> p j t"))
+
+        def quantise_y(c):
+            cols = slice(P * c, P * (c + 1))
+            nc.vector.quantize_mx(
+                out=y_codes[:, cols].bitcast(FP8X4), scales=y_scales[:, cols], in_=y_round[c][:].rearrange("p j t -> p (j t)")
+            )
+            if c % 2 == 1:
+                pair = slice(P * (c - 1), P * (c + 1))
+                nc.sync.dma_start(out_words[:, pair], y_codes[:, pair])
+
+        stages = [score, weigh, turn, quantise_z, values, round_y, quantise_y]
+        for step in range(TILES + len(stages) - 1):
+            for s in reversed(range(len(stages))):
+                if 0 <= step - s < TILES:
+                    stages[s](step - s)
+
+        for q in range(4):
+            queue = nc.scalar if q % 2 == 0 else nc.sync
+            queue.dma_start(out_2[0, 4 * q : 4 * q + 4, :].bitcast(I32), y_scales[32 * q : 32 * q + 4, :].bitcast(I32))

@@ -33,12 +33,14 @@ def tile_picked_rpqscore_relu_po_kernel(
         offs_t = keep.tile([P, S // 16], U16, name="offs_t")
         k1_t = keep.tile([P, H // 16], U16, name="k1_t")
         k2_t = keep.tile([P, H // 16], U16, name="k2_t")
-        x_table = keep.tile([P, T], I32, name="x_table", align_bytes=64)
+        x_table = keep.tile([P, T], I32, name="x_table", tag="x_table", align_bytes=64)
         d_table = keep.tile([P, G], I32, name="d_table", align_bytes=64)
         xs_table = keep.tile([P, T], U8, name="xs_table", align_bytes=64)
         ds_table = keep.tile([P, G], U8, name="ds_table", align_bytes=64)
-        picked_scales = keep.tile([P, 2 * H + S], U8, name="picked_scales", align_bytes=64)
-        planes = keep.tile([P, 2 * H + S], U8, name="planes", align_bytes=64)
+        picked_scales = keep.tile([P, H + S], U8, name="picked_scales", align_bytes=64)
+        planes = keep.tile([P, H + S], U8, name="planes", align_bytes=64)
+        picked_d1 = keep.tile([P, H], U8, name="picked_d1", align_bytes=64)
+        d1_plane = keep.tile([P, H], U8, name="d1_plane", align_bytes=64)
         w_raw = keep.tile([P, 2 * N], U8, name="w_raw", align_bytes=64)
         w_dealt = keep.tile([P, 2 * N], U8, name="w_dealt", align_bytes=64)
         ws_raw = keep.tile([P, N], U8, name="ws_raw", align_bytes=64)
@@ -47,67 +49,75 @@ def tile_picked_rpqscore_relu_po_kernel(
         g_rows = keep.tile([P, 2, P, 2], F32, name="g_rows", align_bytes=64)
         ident = keep.tile([P, P], F32, name="ident")
 
-        nc.vector.memset(xs_table[:].bitcast(I32), 0)
+        ws_plane = keep.tile([P, N], U8, name="ws_plane", align_bytes=64)
+        nc.vector.memset(xs_table[:, 0 : T // 2].bitcast(I32), 0)
+        nc.gpsimd.memset(xs_table[:, T // 2 :].bitcast(I32), 0)
         nc.vector.memset(planes[:].bitcast(I32), 0)
-        nc.vector.memset(ws_raw[:].bitcast(I32), 0)
+        nc.vector.memset(d1_plane[:].bitcast(I32), 0)
+        nc.vector.memset(ws_plane[:].bitcast(I32), 0)
         make_identity(nc, ident[:])
 
         nc.sync.dma_start(k2_t[:], k2)
         nc.sync.dma_start(ds_table[:].bitcast(I32), d_scales[0].bitcast(I32).unsqueeze(1).to_broadcast([16, 8, G // 4]))
         nc.sync.dma_start(xs_table[0:P:8, :].bitcast(I32), x_scales[0].bitcast(I32))
-        nc.sync.dma_start(k1_t[:], k1)
         nc.sync.dma_start(offs_t[:], offs)
-        nc.sync.dma_start(g_cols[:], gn.rearrange("(p t) o -> p (t o)", t=4))
-        nc.sync.dma_start(x_table[:], x_words[0].rearrange("p n t -> p (n t)").bitcast(I32))
+        nc.sync.dma_start(k1_t[:], k1)
+        nc.scalar.dma_start(g_cols[:], gn.rearrange("(p t) o -> p (t o)", t=4))
         nc.sync.dma_start(d_table[:], d_words[0].rearrange("p n t -> p (n t)").bitcast(I32))
+        nc.sync.dma_start(x_table[:], x_words[0].rearrange("p n t -> p (n t)").bitcast(I32))
+        nc.sync.dma_start(ws_raw[:].bitcast(I32), w1_scales[0].bitcast(I32).unsqueeze(1).to_broadcast([16, 8, N // 4]))
         nc.sync.dma_start(w_raw[:].bitcast(I32), w1_words[0].bitcast(I32))
-        for q in range(4):
-            nc.gpsimd.dma_start(ws_raw[32 * q : 32 * q + 4, :].bitcast(I32), w1_scales[0, 4 * q : 4 * q + 4, :].bitcast(I32))
 
-        g_bank = psum.tile([P, 4, P], F32, name="g_bank", tag="out_bank", bufs=2)
+        g_bank = psum.tile([P, 4, P], F32, name="g_bank", tag="spare")
         for t in range(4):
             nc.tensor.transpose(g_bank[:, t, :], g_cols[:, t : t + 1].to_broadcast([P, P]), ident[:])
         nc.scalar.activation(g_rows[:], g_bank[:].rearrange("p (u e) m -> p u m e", e=2), ACT.Copy, scale=0.03125)
 
         nc.vector.tensor_copy(picked_scales[:, 0:H], ds_table[:].indirect(k2_t[:]))
-        nc.vector.tensor_copy(picked_scales[:, H : 2 * H], ds_table[:].indirect(k1_t[:]))
-        nc.vector.tensor_copy(picked_scales[:, 2 * H :], xs_table[:].indirect(offs_t[:]))
+        nc.vector.tensor_copy(picked_scales[:, H : H + S], xs_table[:].indirect(offs_t[:]))
+        nc.vector.tensor_copy(picked_d1[:], ds_table[:].indirect(k1_t[:]))
         for q in range(4):
-            nc.scalar.dma_start(
-                planes[32 * q : 32 * q + 4, :].bitcast(I32), picked_scales[32 * q : 32 * q + 32 : 8, :].bitcast(I32)
-            )
+            queue = nc.scalar if q % 2 == 0 else nc.sync
+            queue.dma_start(planes[32 * q : 32 * q + 4, :].bitcast(I32), picked_scales[32 * q : 32 * q + 32 : 8, :].bitcast(I32))
+        for q in range(4):
+            nc.sync.dma_start(d1_plane[32 * q : 32 * q + 4, :].bitcast(I32), picked_d1[32 * q : 32 * q + 32 : 8, :].bitcast(I32))
         d2_scale = planes[:, 0:H]
-        d1_scale = planes[:, H : 2 * H]
+        d1_scale = d1_plane[:]
 
-        nc.gpsimd.tensor_copy(
-            w_dealt[:].rearrange("p (t m b) -> p t m b", t=4, b=2), w_raw[:].rearrange("p (m t b) -> p t m b", t=4, b=2)
-        )
-        nc.gpsimd.tensor_copy(ws_dealt[:].rearrange("p (t m) -> p t m", t=4), ws_raw[:].rearrange("p (m t) -> p t m", t=4))
 
         d2 = keep.tile([P, H], U32, name="d2", align_bytes=64)
-        d1 = keep.tile([P, H], U32, name="d1", align_bytes=64)
-        xq = keep.tile([P, S], U32, name="xq", align_bytes=64)
-        nc.vector.tensor_copy(xq[:], x_table[:].bitcast(U32).indirect(offs_t[:]))
+        xq = [keep.tile([P, HALF], U32, name=f"xq{h}", align_bytes=64) for h in range(2)]
         nc.vector.tensor_copy(d2[:], d_table[:].bitcast(U32).indirect(k2_t[:]))
+        for h in range(2):
+            nc.vector.tensor_copy(xq[h][:], x_table[:].bitcast(U32).indirect(offs_t[:, 16 * h : 16 * (h + 1)]))
+        d1 = keep.tile([P, H], U32, name="d1", tag="x_table", align_bytes=64)
         nc.vector.tensor_copy(d1[:], d_table[:].bitcast(U32).indirect(k1_t[:]))
+
+        nc.vector.tensor_copy(ws_dealt[:].rearrange("p (t m) -> p t m", t=4), ws_raw[:].rearrange("p (m t) -> p t m", t=4))
+        for q in range(4):
+            nc.sync.dma_start(ws_plane[32 * q : 32 * q + 4, :].bitcast(I32), ws_dealt[32 * q : 32 * q + 32 : 8, :].bitcast(I32))
+        nc.vector.tensor_copy(
+            w_dealt[:].rearrange("p (t m b) -> p t m b", t=4, b=2), w_raw[:].rearrange("p (m t b) -> p t m b", t=4, b=2)
+        )
 
         def score_pass(bank, c, keys, key_scale, start, stop):
             nc.tensor.matmul_mx(
                 out=bank[:],
-                lhsT=xq[:, P * c : P * (c + 1)].bitcast(FP8X4),
-                lhsT_scale=planes[:, 2 * H + P * c : 2 * H + P * (c + 1)],
+                lhsT=xq[c // 2][:, P * (c % 2) : P * (c % 2 + 1)].bitcast(FP8X4),
+                lhsT_scale=planes[:, H + P * c : H + P * (c + 1)],
                 rhs=keys[:].bitcast(FP8X4),
                 rhs_scale=key_scale,
                 start=start,
                 stop=stop,
             )
 
-        fine_bank = psum.tile([P, H], F32, name="fine_bank", tag="out_bank", bufs=2)
+        fine_bank = psum.tile([P, H], F32, name="fine_bank", tag="fine")
         score_pass(fine_bank, 0, d2, d2_scale, True, True)
         fine = keep.tile([P, H], F32, name="fine")
         nc.scalar.copy(fine[:], fine_bank[:])
         banks = [psum.tile([P, H], F32, name=f"score{c}", tag=f"score{c}") for c in range(TILES)]
-        score_pass(banks[1], 1, d2, d2_scale, True, False)
+        for c in (1, 2):
+            score_pass(banks[c], c, d2, d2_scale, True, False)
         summed = keep.tile([P, H], F32, name="summed")
         scores = [summed] + banks[1:]
 
@@ -128,7 +138,7 @@ def tile_picked_rpqscore_relu_po_kernel(
                 score_pass(banks[0], 0, d1, d1_scale, True, True)
                 nc.vector.scalar_tensor_tensor(summed[:], banks[0][:], 2.0, fine[:], ALU.mult, ALU.add)
             else:
-                if c > 1:
+                if c > 2:
                     score_pass(banks[c], c, d2, d2_scale, True, False)
                 score_pass(banks[c], c, d1, d1_scale, False, False)
                 score_pass(banks[c], c, d1, d1_scale, False, True)
@@ -154,18 +164,27 @@ def tile_picked_rpqscore_relu_po_kernel(
             )
 
         def values(c):
-            bank = psum.tile([P, 4, P], F32, name="out_bank", tag="out_bank", bufs=2)
+            if c < TILES - 1:
+                bank = psum.tile([P, 4, P], F32, name="out_bank", tag=f"score{c}")
+                slots = [bank[:, t, :] for t in range(4)]
+            else:
+                pair = [psum.tile([P, 2, P], F32, name=tag, tag=tag) for tag in ("spare", "fine")]
+                slots = [pair[t // 2][:, t % 2, :] for t in range(4)]
             for t in range(4):
                 nc.tensor.matmul_mx(
-                    out=bank[:, t, :],
+                    out=slots[t],
                     lhsT=w_dealt[:, 2 * P * t : 2 * P * (t + 1)].bitcast(FP4X4),
-                    lhsT_scale=ws_dealt[:, P * t : P * (t + 1)],
+                    lhsT_scale=ws_plane[:, P * t : P * (t + 1)],
                     rhs=z_codes[c][:].bitcast(FP8X4),
                     rhs_scale=z_scales[c][:],
                     start=True,
                     stop=True,
                 )
-            nc.scalar.copy(y[c][:], bank[:])
+            if c < TILES - 1:
+                nc.scalar.copy(y[c][:], bank[:])
+            else:
+                nc.scalar.copy(y[c][:, 0:2], pair[0][:])
+                nc.vector.tensor_copy(y[c][:, 2:4], pair[1][:])
             nc.sync.dma_start(out_rows[:, :, P * c : P * (c + 1)], y[c][:])
 
         def round_y(c):
@@ -180,7 +199,11 @@ def tile_picked_rpqscore_relu_po_kernel(
                 pair = slice(P * (c - 1), P * (c + 1))
                 nc.sync.dma_start(out_words[:, pair], y_codes[:, pair])
 
-        stages = [score, weigh, turn, quantise_z, values, round_y, quantise_y]
+        for c in range(TILES):
+            score(c)
+        for c in range(TILES):
+            weigh(c)
+        stages = [turn, quantise_z, values, round_y, quantise_y]
         for step in range(TILES + len(stages) - 1):
             for s in reversed(range(len(stages))):
                 if 0 <= step - s < TILES:

@@ -77,8 +77,7 @@ def tile_picked_rpqscore_relu_po_kernel(
         nc.vector.tensor_copy(picked_scales[:, H : H + S], xs_table[:].indirect(offs_t[:]))
         nc.vector.tensor_copy(picked_d1[:], ds_table[:].indirect(k1_t[:]))
         for q in range(4):
-            queue = nc.scalar if q % 2 == 0 else nc.sync
-            queue.dma_start(planes[32 * q : 32 * q + 4, :].bitcast(I32), picked_scales[32 * q : 32 * q + 32 : 8, :].bitcast(I32))
+            nc.scalar.dma_start(planes[32 * q : 32 * q + 4, :].bitcast(I32), picked_scales[32 * q : 32 * q + 32 : 8, :].bitcast(I32))
         for q in range(4):
             nc.sync.dma_start(d1_plane[32 * q : 32 * q + 4, :].bitcast(I32), picked_d1[32 * q : 32 * q + 32 : 8, :].bitcast(I32))
         d2_scale = planes[:, 0:H]
@@ -195,9 +194,9 @@ def tile_picked_rpqscore_relu_po_kernel(
             nc.vector.quantize_mx(
                 out=y_codes[:, cols].bitcast(FP8X4), scales=y_scales[:, cols], in_=y_round[c][:].rearrange("p j t -> p (j t)")
             )
-            if c % 2 == 1:
-                pair = slice(P * (c - 1), P * (c + 1))
-                nc.sync.dma_start(out_words[:, pair], y_codes[:, pair])
+            if c >= TILES - 2:
+                done = slice(0, P * (c + 1)) if c == TILES - 2 else cols
+                nc.sync.dma_start(out_words[:, done], y_codes[:, done])
 
         for c in range(TILES):
             score(c)

@@ -34,7 +34,7 @@ def tile_picked_rpqscore_relu_po_kernel(
         k1_t = keep.tile([P, H // 16], U16, name="k1_t")
         k2_t = keep.tile([P, H // 16], U16, name="k2_t")
         x_table = keep.tile([P, T], I32, name="x_table", tag="x_table", align_bytes=64)
-        d_table = keep.tile([P, G], I32, name="d_table", align_bytes=64)
+        d_table = keep.tile([P, G], I32, name="d_table", tag="d_table", align_bytes=64)
         xs_table = keep.tile([P, T], U8, name="xs_table", align_bytes=64)
         ds_table = keep.tile([P, G], U8, name="ds_table", align_bytes=64)
         picked_scales = keep.tile([P, H + S], U8, name="picked_scales", align_bytes=64)
@@ -42,7 +42,6 @@ def tile_picked_rpqscore_relu_po_kernel(
         picked_d1 = keep.tile([P, H], U8, name="picked_d1", align_bytes=64)
         d1_plane = keep.tile([P, H], U8, name="d1_plane", align_bytes=64)
         w_raw = keep.tile([P, 2 * N], U8, name="w_raw", align_bytes=64)
-        w_dealt = keep.tile([P, 2 * N], U8, name="w_dealt", align_bytes=64)
         ws_raw = keep.tile([P, N], U8, name="ws_raw", align_bytes=64)
         ws_dealt = keep.tile([P, N], U8, name="ws_dealt", align_bytes=64)
         g_cols = keep.tile([P, 4], F32, name="g_cols")
@@ -50,23 +49,24 @@ def tile_picked_rpqscore_relu_po_kernel(
         ident = keep.tile([P, P], F32, name="ident")
 
         ws_plane = keep.tile([P, N], U8, name="ws_plane", align_bytes=64)
-        nc.vector.memset(xs_table[:, 0 : T // 2].bitcast(I32), 0)
-        nc.gpsimd.memset(xs_table[:, T // 2 :].bitcast(I32), 0)
+        nc.vector.memset(ds_table[:].bitcast(I32), 0)
+        nc.gpsimd.memset(xs_table[:].bitcast(I32), 0)
+        nc.vector.memset(ws_raw[:].bitcast(I32), 0)
         nc.vector.memset(planes[:].bitcast(I32), 0)
         nc.vector.memset(d1_plane[:].bitcast(I32), 0)
         nc.vector.memset(ws_plane[:].bitcast(I32), 0)
         make_identity(nc, ident[:])
 
         nc.sync.dma_start(k2_t[:], k2)
-        nc.sync.dma_start(ds_table[:].bitcast(I32), d_scales[0].bitcast(I32).unsqueeze(1).to_broadcast([16, 8, G // 4]))
+        nc.sync.dma_start(ds_table[0:P:8, :].bitcast(I32), d_scales[0].bitcast(I32))
         nc.sync.dma_start(xs_table[0:P:8, :].bitcast(I32), x_scales[0].bitcast(I32))
         nc.sync.dma_start(offs_t[:], offs)
         nc.sync.dma_start(k1_t[:], k1)
-        nc.scalar.dma_start(g_cols[:], gn.rearrange("(p t) o -> p (t o)", t=4))
+        nc.sync.dma_start(g_cols[:], gn.rearrange("(p t) o -> p (t o)", t=4))
+        nc.sync.dma_start(w_raw[:].bitcast(I32), w1_words[0].bitcast(I32))
         nc.sync.dma_start(d_table[:], d_words[0].rearrange("p n t -> p (n t)").bitcast(I32))
         nc.sync.dma_start(x_table[:], x_words[0].rearrange("p n t -> p (n t)").bitcast(I32))
-        nc.sync.dma_start(ws_raw[:].bitcast(I32), w1_scales[0].bitcast(I32).unsqueeze(1).to_broadcast([16, 8, N // 4]))
-        nc.sync.dma_start(w_raw[:].bitcast(I32), w1_words[0].bitcast(I32))
+        nc.sync.dma_start(ws_raw[0:P:8, :].bitcast(I32), w1_scales[0].bitcast(I32))
 
         g_bank = psum.tile([P, 4, P], F32, name="g_bank", tag="spare")
         for t in range(4):
@@ -95,6 +95,7 @@ def tile_picked_rpqscore_relu_po_kernel(
         nc.vector.tensor_copy(ws_dealt[:].rearrange("p (t m) -> p t m", t=4), ws_raw[:].rearrange("p (m t) -> p t m", t=4))
         for q in range(4):
             nc.sync.dma_start(ws_plane[32 * q : 32 * q + 4, :].bitcast(I32), ws_dealt[32 * q : 32 * q + 32 : 8, :].bitcast(I32))
+        w_dealt = keep.tile([P, 2 * N], U8, name="w_dealt", tag="d_table", align_bytes=64)
         nc.vector.tensor_copy(
             w_dealt[:].rearrange("p (t m b) -> p t m b", t=4, b=2), w_raw[:].rearrange("p (m t b) -> p t m b", t=4, b=2)
         )
@@ -163,11 +164,11 @@ def tile_picked_rpqscore_relu_po_kernel(
             )
 
         def values(c):
-            if c < TILES - 1:
+            if c < 2:
                 bank = psum.tile([P, 4, P], F32, name="out_bank", tag=f"score{c}")
                 slots = [bank[:, t, :] for t in range(4)]
             else:
-                pair = [psum.tile([P, 2, P], F32, name=tag, tag=tag) for tag in ("spare", "fine")]
+                pair = [psum.tile([P, 2, P], F32, name="out_pair", tag=tag) for tag in (("score2", "score3") if c == 2 else ("spare", "fine"))]
                 slots = [pair[t // 2][:, t % 2, :] for t in range(4)]
             for t in range(4):
                 nc.tensor.matmul_mx(
@@ -179,7 +180,7 @@ def tile_picked_rpqscore_relu_po_kernel(
                     start=True,
                     stop=True,
                 )
-            if c < TILES - 1:
+            if c < 2:
                 nc.scalar.copy(y[c][:], bank[:])
             else:
                 nc.scalar.copy(y[c][:, 0:2], pair[0][:])
@@ -198,11 +199,7 @@ def tile_picked_rpqscore_relu_po_kernel(
                 done = slice(0, P * (c + 1)) if c == TILES - 2 else cols
                 nc.sync.dma_start(out_words[:, done], y_codes[:, done])
 
-        for c in range(TILES):
-            score(c)
-        for c in range(TILES):
-            weigh(c)
-        stages = [turn, quantise_z, values, round_y, quantise_y]
+        stages = [score, weigh, turn, quantise_z, values, round_y, quantise_y]
         for step in range(TILES + len(stages) - 1):
             for s in reversed(range(len(stages))):
                 if 0 <= step - s < TILES:

@@ -19,6 +19,7 @@ ACT = mybir.ActivationFunctionType
 
 P = 128
 TILES = S // P
+LAST = TILES - 1
 HALF = S // 2
 
 
@@ -28,77 +29,76 @@ def tile_picked_rpqscore_relu_po_kernel(
     nc = tc.nc
     with ExitStack() as ctx:
         keep = ctx.enter_context(tc.tile_pool(name="keep", bufs=1))
+        shared = ctx.enter_context(tc.tile_pool(name="shared", bufs=1))
         psum = ctx.enter_context(tc.psum_pool(name="psum", bufs=1))
 
         offs_t = keep.tile([P, S // 16], U16, name="offs_t")
         k1_t = keep.tile([P, H // 16], U16, name="k1_t")
         k2_t = keep.tile([P, H // 16], U16, name="k2_t")
-        x_table = keep.tile([P, T], I32, name="x_table", tag="x_table", align_bytes=64)
-        d_table = keep.tile([P, G], I32, name="d_table", tag="d_table", align_bytes=64)
+        x_table = shared.tile([P, T], I32, name="x_table", align_bytes=64, offset=0)
+        d_table = keep.tile([P, G], I32, name="d_table", align_bytes=64)
         xs_table = keep.tile([P, T], U8, name="xs_table", align_bytes=64)
-        ds_table = keep.tile([P, G], U8, name="ds_table", align_bytes=64)
+        ds_table = shared.tile([P, G], U8, name="ds_table", align_bytes=64, offset=4 * T)
         picked_scales = keep.tile([P, H + S], U8, name="picked_scales", align_bytes=64)
         planes = keep.tile([P, H + S], U8, name="planes", align_bytes=64)
         picked_d1 = keep.tile([P, H], U8, name="picked_d1", align_bytes=64)
         d1_plane = keep.tile([P, H], U8, name="d1_plane", align_bytes=64)
         w_raw = keep.tile([P, 2 * N], U8, name="w_raw", align_bytes=64)
-        ws_raw = keep.tile([P, N], U8, name="ws_raw", align_bytes=64)
-        ws_dealt = keep.tile([P, N], U8, name="ws_dealt", align_bytes=64)
+        g_raw = keep.tile([P, 4], F32, name="g_raw")
         g_cols = keep.tile([P, 4], F32, name="g_cols")
         g_rows = keep.tile([P, 2, P, 2], F32, name="g_rows", align_bytes=64)
         ident = keep.tile([P, P], F32, name="ident")
 
-        ws_plane = keep.tile([P, N], U8, name="ws_plane", align_bytes=64)
-        nc.vector.memset(ds_table[:].bitcast(I32), 0)
-        nc.gpsimd.memset(xs_table[:].bitcast(I32), 0)
-        nc.vector.memset(ws_raw[:].bitcast(I32), 0)
+        nc.vector.memset(xs_table[:].bitcast(I32), 0)
+        nc.vector.memset(ds_table[:, 0 : G // 2].bitcast(I32), 0)
+        nc.gpsimd.memset(ds_table[:, G // 2 : G].bitcast(I32), 0)
         nc.vector.memset(planes[:].bitcast(I32), 0)
         nc.vector.memset(d1_plane[:].bitcast(I32), 0)
-        nc.vector.memset(ws_plane[:].bitcast(I32), 0)
         make_identity(nc, ident[:])
 
-        nc.sync.dma_start(k2_t[:], k2)
-        nc.sync.dma_start(ds_table[0:P:8, :].bitcast(I32), d_scales[0].bitcast(I32))
-        nc.sync.dma_start(xs_table[0:P:8, :].bitcast(I32), x_scales[0].bitcast(I32))
         nc.sync.dma_start(offs_t[:], offs)
+        nc.sync.dma_start(k2_t[:], k2)
         nc.sync.dma_start(k1_t[:], k1)
-        nc.sync.dma_start(g_cols[:], gn.rearrange("(p t) o -> p (t o)", t=4))
-        nc.sync.dma_start(w_raw[:].bitcast(I32), w1_words[0].bitcast(I32))
+        nc.sync.dma_start(g_raw[:], gn.rearrange("(p t) o -> p (t o)", t=4))
+        nc.sync.dma_start(xs_table[0:P:8, :].bitcast(I32), x_scales[0].bitcast(I32))
+        nc.sync.dma_start(ds_table[0:P:8, :].bitcast(I32), d_scales[0].bitcast(I32))
         nc.sync.dma_start(d_table[:], d_words[0].rearrange("p n t -> p (n t)").bitcast(I32))
         nc.sync.dma_start(x_table[:], x_words[0].rearrange("p n t -> p (n t)").bitcast(I32))
-        nc.sync.dma_start(ws_raw[0:P:8, :].bitcast(I32), w1_scales[0].bitcast(I32))
+        nc.sync.dma_start(w_raw[:].bitcast(I32), w1_words[0].bitcast(I32))
 
+        nc.scalar.activation(g_cols[:], g_raw[:], ACT.Copy, scale=0.03125)
         g_bank = psum.tile([P, 4, P], F32, name="g_bank", tag="spare")
         for t in range(4):
-            nc.tensor.transpose(g_bank[:, t, :], g_cols[:, t : t + 1].to_broadcast([P, P]), ident[:])
+            nc.tensor.transpose(g_bank[:, t, :], g_raw[:, t : t + 1].to_broadcast([P, P]), ident[:])
         nc.scalar.activation(g_rows[:], g_bank[:].rearrange("p (u e) m -> p u m e", e=2), ACT.Copy, scale=0.03125)
 
-        nc.vector.tensor_copy(picked_scales[:, 0:H], ds_table[:].indirect(k2_t[:]))
         nc.vector.tensor_copy(picked_scales[:, H : H + S], xs_table[:].indirect(offs_t[:]))
+        nc.vector.tensor_copy(picked_scales[:, 0:H], ds_table[:].indirect(k2_t[:]))
         nc.vector.tensor_copy(picked_d1[:], ds_table[:].indirect(k1_t[:]))
         for q in range(4):
-            nc.scalar.dma_start(planes[32 * q : 32 * q + 4, :].bitcast(I32), picked_scales[32 * q : 32 * q + 32 : 8, :].bitcast(I32))
+            queue = nc.scalar if q % 2 == 0 else nc.sync
+            queue.dma_start(planes[32 * q : 32 * q + 4, :].bitcast(I32), picked_scales[32 * q : 32 * q + 32 : 8, :].bitcast(I32))
+        ws_raw = shared.tile([P, N], U8, name="ws_raw", align_bytes=64, offset=4 * T)
         for q in range(4):
             nc.sync.dma_start(d1_plane[32 * q : 32 * q + 4, :].bitcast(I32), picked_d1[32 * q : 32 * q + 32 : 8, :].bitcast(I32))
-        d2_scale = planes[:, 0:H]
-        d1_scale = d1_plane[:]
-
+        for q in range(4):
+            rows = w1_scales[0, 4 * q : 4 * q + 4, :].bitcast(I32)
+            nc.sync.dma_start(ws_raw[32 * q : 32 * q + 32, :].bitcast(I32), rows.unsqueeze(0).to_broadcast([8, 4, N // 4]))
 
         d2 = keep.tile([P, H], U32, name="d2", align_bytes=64)
         xq = [keep.tile([P, HALF], U32, name=f"xq{h}", align_bytes=64) for h in range(2)]
         nc.vector.tensor_copy(d2[:], d_table[:].bitcast(U32).indirect(k2_t[:]))
         for h in range(2):
             nc.vector.tensor_copy(xq[h][:], x_table[:].bitcast(U32).indirect(offs_t[:, 16 * h : 16 * (h + 1)]))
-        d1 = keep.tile([P, H], U32, name="d1", tag="x_table", align_bytes=64)
+        d1 = shared.tile([P, H], U32, name="d1", align_bytes=64, offset=0)
         nc.vector.tensor_copy(d1[:], d_table[:].bitcast(U32).indirect(k1_t[:]))
 
-        nc.vector.tensor_copy(ws_dealt[:].rearrange("p (t m) -> p t m", t=4), ws_raw[:].rearrange("p (m t) -> p t m", t=4))
-        for q in range(4):
-            nc.sync.dma_start(ws_plane[32 * q : 32 * q + 4, :].bitcast(I32), ws_dealt[32 * q : 32 * q + 32 : 8, :].bitcast(I32))
-        w_dealt = keep.tile([P, 2 * N], U8, name="w_dealt", tag="d_table", align_bytes=64)
-        nc.vector.tensor_copy(
+        w_dealt = shared.tile([P, 2 * N], U8, name="w_dealt", align_bytes=64, offset=4 * H)
+        w_plane = shared.tile([P, N], U8, name="w_plane", align_bytes=64, offset=4 * H + 2 * N)
+        nc.gpsimd.tensor_copy(
             w_dealt[:].rearrange("p (t m b) -> p t m b", t=4, b=2), w_raw[:].rearrange("p (m t b) -> p t m b", t=4, b=2)
         )
+        nc.gpsimd.tensor_copy(w_plane[:].rearrange("p (t m) -> p t m", t=4), ws_raw[:].rearrange("p (m t) -> p t m", t=4))
 
         def score_pass(bank, c, keys, key_scale, start, stop):
             nc.tensor.matmul_mx(
@@ -111,40 +111,40 @@ def tile_picked_rpqscore_relu_po_kernel(
                 stop=stop,
             )
 
-        fine_bank = psum.tile([P, H], F32, name="fine_bank", tag="fine")
-        score_pass(fine_bank, 0, d2, d2_scale, True, True)
-        fine = keep.tile([P, H], F32, name="fine")
-        nc.scalar.copy(fine[:], fine_bank[:])
         banks = [psum.tile([P, H], F32, name=f"score{c}", tag=f"score{c}") for c in range(TILES)]
-        for c in (1, 2):
-            score_pass(banks[c], c, d2, d2_scale, True, False)
-        summed = keep.tile([P, H], F32, name="summed")
-        scores = [summed] + banks[1:]
+        fine_bank = psum.tile([P, H], F32, name="fine_bank", tag="fine")
+        fine = keep.tile([P, 4, P], F32, name="fine", align_bytes=64)
+        coarse = keep.tile([P, 4, P], F32, name="coarse", align_bytes=64)
+        for c in range(LAST - 1):
+            score_pass(banks[c], c, d2, planes[:, 0:H], True, False)
+        score_pass(fine_bank, LAST, d2, planes[:, 0:H], True, True)
+        nc.scalar.copy(fine[:], fine_bank[:].rearrange("p (m t) -> p t m", t=4))
 
         y_codes = keep.tile([P, S], I32, name="y_codes", align_bytes=64)
         y_scales = keep.tile([P, S], U8, name="y_scales", align_bytes=64)
         out_rows = out_0.rearrange("(p t) j -> p t j", t=4)
         out_words = out_1[0].rearrange("p j t -> p (j t)").bitcast(I32)
 
-        z_rows = [keep.tile([P, 2, P, 2], BF16, name=f"z_rows{c}", align_bytes=64) for c in range(TILES)]
+        z_rows = [keep.tile([P, 2, P, 2], BF16, name=f"z_rows{c}", align_bytes=64) for c in range(LAST)]
         z_cols = [keep.tile([P, P, 4], BF16, name=f"z_cols{c}", align_bytes=64) for c in range(TILES)]
         z_codes = [keep.tile([P, P], U32, name=f"z_codes{c}", align_bytes=64) for c in range(TILES)]
         z_scales = [keep.tile([P, P], U8, name=f"z_scales{c}", align_bytes=64) for c in range(TILES)]
         y = [keep.tile([P, 4, P], F32, name=f"y{c}", align_bytes=64) for c in range(TILES)]
-        y_round = [keep.tile([P, P, 4], BF16, name=f"y_round{c}", align_bytes=64) for c in range(TILES)]
+        early_round = keep.tile([P, 2 * P, 4], BF16, name="early_round", align_bytes=64)
+        late_round = [keep.tile([P, P, 4], BF16, name=f"late_round{c}", align_bytes=64) for c in range(2)]
+        y_round = [early_round[:, 0:P], early_round[:, P : 2 * P], late_round[0][:], late_round[1][:]]
 
         def score(c):
-            if c == 0:
-                score_pass(banks[0], 0, d1, d1_scale, True, True)
-                nc.vector.scalar_tensor_tensor(summed[:], banks[0][:], 2.0, fine[:], ALU.mult, ALU.add)
-            else:
-                if c > 2:
-                    score_pass(banks[c], c, d2, d2_scale, True, False)
-                score_pass(banks[c], c, d1, d1_scale, False, False)
-                score_pass(banks[c], c, d1, d1_scale, False, True)
+            if c == LAST - 1:
+                score_pass(banks[c], c, d2, planes[:, 0:H], True, False)
+            score_pass(banks[c], c, d1, d1_plane[:], False, False)
+            score_pass(banks[c], c, d1, d1_plane[:], False, True)
+            if c == 1:
+                score_pass(banks[LAST], LAST, d1, d1_plane[:], True, True)
+                nc.scalar.activation(coarse[:], banks[LAST][:].rearrange("p (m t) -> p t m", t=4), ACT.Copy, scale=2.0)
 
         def weigh(c):
-            view = scores[c][:].rearrange("p (m u e) -> p u m e", u=2, e=2)
+            view = banks[c][:].rearrange("p (m u e) -> p u m e", u=2, e=2)
             for u in range(2):
                 nc.vector.scalar_tensor_tensor(z_rows[c][:, u], view[:, u], 0.0, g_rows[:, u], ALU.max, ALU.mult)
 
@@ -158,6 +158,23 @@ def tile_picked_rpqscore_relu_po_kernel(
                 turned[:].rearrange("p u j -> p j u"),
             )
 
+        summed = psum.tile([P, 4, P], F32, name="summed", tag="fine")
+
+        def turn_last():
+            for t in range(4):
+                nc.tensor.matmul(summed[:, t, :], fine[:, t, :], ident[:], start=True, stop=False, is_transpose=True)
+                nc.tensor.matmul(summed[:, t, :], coarse[:, t, :], ident[:], start=False, stop=True, is_transpose=True)
+
+        def weigh_last():
+            nc.vector.scalar_tensor_tensor(
+                z_cols[LAST][:],
+                summed[:].rearrange("p t j -> p j t"),
+                0.0,
+                g_cols[:].unsqueeze(1).to_broadcast([P, P, 4]),
+                ALU.max,
+                ALU.mult,
+            )
+
         def quantise_z(c):
             nc.vector.quantize_mx(
                 out=z_codes[c][:].bitcast(FP8X4), scales=z_scales[c][:], in_=z_cols[c][:].rearrange("p j t -> p (j t)")
@@ -168,13 +185,13 @@ def tile_picked_rpqscore_relu_po_kernel(
                 bank = psum.tile([P, 4, P], F32, name="out_bank", tag=f"score{c}")
                 slots = [bank[:, t, :] for t in range(4)]
             else:
-                pair = [psum.tile([P, 2, P], F32, name="out_pair", tag=tag) for tag in (("score2", "score3") if c == 2 else ("spare", "fine"))]
+                pair = [psum.tile([P, 2, P], F32, name="out_pair", tag=tag) for tag in (("score2", "spare") if c == 2 else ("score3", "score0"))]
                 slots = [pair[t // 2][:, t % 2, :] for t in range(4)]
             for t in range(4):
                 nc.tensor.matmul_mx(
                     out=slots[t],
                     lhsT=w_dealt[:, 2 * P * t : 2 * P * (t + 1)].bitcast(FP4X4),
-                    lhsT_scale=ws_plane[:, P * t : P * (t + 1)],
+                    lhsT_scale=w_plane[:, P * t : P * (t + 1)],
                     rhs=z_codes[c][:].bitcast(FP8X4),
                     rhs_scale=z_scales[c][:],
                     start=True,
@@ -188,18 +205,29 @@ def tile_picked_rpqscore_relu_po_kernel(
             nc.sync.dma_start(out_rows[:, :, P * c : P * (c + 1)], y[c][:])
 
         def round_y(c):
-            nc.vector.tensor_copy(y_round[c][:], y[c][:].rearrange("p t j -> p j t"))
+            nc.vector.tensor_copy(y_round[c], y[c][:].rearrange("p t j -> p j t"))
 
         def quantise_y(c):
-            cols = slice(P * c, P * (c + 1))
+            if c == 0:
+                return
+            cols = slice(0, 2 * P) if c == 1 else slice(P * c, P * (c + 1))
+            rounded = early_round[:] if c == 1 else y_round[c]
             nc.vector.quantize_mx(
-                out=y_codes[:, cols].bitcast(FP8X4), scales=y_scales[:, cols], in_=y_round[c][:].rearrange("p j t -> p (j t)")
+                out=y_codes[:, cols].bitcast(FP8X4), scales=y_scales[:, cols], in_=rounded.rearrange("p j t -> p (j t)")
             )
             if c >= TILES - 2:
                 done = slice(0, P * (c + 1)) if c == TILES - 2 else cols
                 nc.sync.dma_start(out_words[:, done], y_codes[:, done])
 
-        stages = [score, weigh, turn, quantise_z, values, round_y, quantise_y]
+        for c in range(LAST):
+            score(c)
+        for c in range(LAST):
+            weigh(c)
+            turn(c)
+            if c == 0:
+                turn_last()
+        weigh_last()
+        stages = [quantise_z, values, round_y, quantise_y]
         for step in range(TILES + len(stages) - 1):
             for s in reversed(range(len(stages))):
                 if 0 <= step - s < TILES:

@@ -95,10 +95,10 @@ def tile_picked_rpqscore_relu_po_kernel(
 
         w_dealt = shared.tile([P, 2 * N], U8, name="w_dealt", align_bytes=64, offset=4 * H)
         w_plane = shared.tile([P, N], U8, name="w_plane", align_bytes=64, offset=4 * H + 2 * N)
-        nc.gpsimd.tensor_copy(
+        nc.vector.tensor_copy(
             w_dealt[:].rearrange("p (t m b) -> p t m b", t=4, b=2), w_raw[:].rearrange("p (m t b) -> p t m b", t=4, b=2)
         )
-        nc.gpsimd.tensor_copy(w_plane[:].rearrange("p (t m) -> p t m", t=4), ws_raw[:].rearrange("p (m t) -> p t m", t=4))
+        nc.vector.tensor_copy(w_plane[:].rearrange("p (t m) -> p t m", t=4), ws_raw[:].rearrange("p (m t) -> p t m", t=4))
 
         def score_pass(bank, c, keys, key_scale, start, stop):
             nc.tensor.matmul_mx(

@@ -21,6 +21,9 @@ P = 128
 TILES = S // P
 LAST = TILES - 1
 HALF = S // 2
+SUMMED = 0
+Z_AT = 2 * H * 4 + 4 * G
+SUM_AT = Z_AT + 2 * H
 
 
 def tile_picked_rpqscore_relu_po_kernel(
@@ -35,17 +38,16 @@ def tile_picked_rpqscore_relu_po_kernel(
         offs_t = keep.tile([P, S // 16], U16, name="offs_t")
         k1_t = keep.tile([P, H // 16], U16, name="k1_t")
         k2_t = keep.tile([P, H // 16], U16, name="k2_t")
-        x_table = shared.tile([P, T], I32, name="x_table", align_bytes=64, offset=0)
-        d_table = keep.tile([P, G], I32, name="d_table", align_bytes=64)
+        x_table = keep.tile([P, T], I32, name="x_table", align_bytes=64)
+        d_table = shared.tile([P, G], I32, name="d_table", align_bytes=64, offset=2 * H * 4)
         xs_table = keep.tile([P, T], U8, name="xs_table", align_bytes=64)
-        ds_table = shared.tile([P, G], U8, name="ds_table", align_bytes=64, offset=4 * T)
-        picked_scales = keep.tile([P, H + S], U8, name="picked_scales", align_bytes=64)
-        planes = keep.tile([P, H + S], U8, name="planes", align_bytes=64)
-        picked_d1 = keep.tile([P, H], U8, name="picked_d1", align_bytes=64)
-        d1_plane = keep.tile([P, H], U8, name="d1_plane", align_bytes=64)
+        ds_table = keep.tile([P, G], U8, name="ds_table", align_bytes=64)
+        picked = shared.tile([P, S + H], U8, name="picked", align_bytes=64, offset=0)
+        planes = keep.tile([P, S + H], U8, name="planes", align_bytes=64)
+        picked_d2 = keep.tile([P, H], U8, name="picked_d2", align_bytes=64)
+        d2_plane = keep.tile([P, H], U8, name="d2_plane", align_bytes=64)
         w_raw = keep.tile([P, 2 * N], U8, name="w_raw", align_bytes=64)
         g_raw = keep.tile([P, 4], F32, name="g_raw")
-        g_cols = keep.tile([P, 4], F32, name="g_cols")
         g_rows = keep.tile([P, 2, P, 2], F32, name="g_rows", align_bytes=64)
         ident = keep.tile([P, P], F32, name="ident")
 
@@ -53,103 +55,110 @@ def tile_picked_rpqscore_relu_po_kernel(
         nc.vector.memset(ds_table[:, 0 : G // 2].bitcast(I32), 0)
         nc.gpsimd.memset(ds_table[:, G // 2 : G].bitcast(I32), 0)
         nc.vector.memset(planes[:].bitcast(I32), 0)
-        nc.vector.memset(d1_plane[:].bitcast(I32), 0)
+        nc.vector.memset(d2_plane[:].bitcast(I32), 0)
         make_identity(nc, ident[:])
 
         nc.sync.dma_start(offs_t[:], offs)
-        nc.sync.dma_start(k2_t[:], k2)
-        nc.sync.dma_start(k1_t[:], k1)
         nc.sync.dma_start(g_raw[:], gn.rearrange("(p t) o -> p (t o)", t=4))
         nc.sync.dma_start(xs_table[0:P:8, :].bitcast(I32), x_scales[0].bitcast(I32))
+        nc.sync.dma_start(k1_t[:], k1)
         nc.sync.dma_start(ds_table[0:P:8, :].bitcast(I32), d_scales[0].bitcast(I32))
+        nc.sync.dma_start(k2_t[:], k2)
         nc.sync.dma_start(d_table[:], d_words[0].rearrange("p n t -> p (n t)").bitcast(I32))
         nc.sync.dma_start(x_table[:], x_words[0].rearrange("p n t -> p (n t)").bitcast(I32))
-        nc.sync.dma_start(w_raw[:].bitcast(I32), w1_words[0].bitcast(I32))
 
-        nc.scalar.activation(g_cols[:], g_raw[:], ACT.Copy, scale=0.03125)
-        g_bank = psum.tile([P, 4, P], F32, name="g_bank", tag="spare")
+        g_scaled = keep.tile([P, 4], F32, name="g_scaled")
+        nc.scalar.activation(g_scaled[:], g_raw[:], ACT.Copy, scale=0.03125)
+        g_bank = psum.tile([P, 4, P], F32, name="g_bank", tag="a")
         for t in range(4):
-            nc.tensor.transpose(g_bank[:, t, :], g_raw[:, t : t + 1].to_broadcast([P, P]), ident[:])
-        nc.scalar.activation(g_rows[:], g_bank[:].rearrange("p (u e) m -> p u m e", e=2), ACT.Copy, scale=0.03125)
+            nc.tensor.transpose(g_bank[:, t, :], g_scaled[:, t : t + 1].to_broadcast([P, P]), ident[:])
+        nc.scalar.copy(g_rows[:], g_bank[:].rearrange("p (u e) m -> p u m e", e=2))
 
-        nc.vector.tensor_copy(picked_scales[:, H : H + S], xs_table[:].indirect(offs_t[:]))
-        nc.vector.tensor_copy(picked_scales[:, 0:H], ds_table[:].indirect(k2_t[:]))
-        nc.vector.tensor_copy(picked_d1[:], ds_table[:].indirect(k1_t[:]))
-        for q in range(4):
-            queue = nc.scalar if q % 2 == 0 else nc.sync
-            queue.dma_start(planes[32 * q : 32 * q + 4, :].bitcast(I32), picked_scales[32 * q : 32 * q + 32 : 8, :].bitcast(I32))
-        ws_raw = shared.tile([P, N], U8, name="ws_raw", align_bytes=64, offset=4 * T)
-        for q in range(4):
-            nc.sync.dma_start(d1_plane[32 * q : 32 * q + 4, :].bitcast(I32), picked_d1[32 * q : 32 * q + 32 : 8, :].bitcast(I32))
+        nc.vector.tensor_copy(picked[:, 0:S], xs_table[:].indirect(offs_t[:]))
+        nc.vector.tensor_copy(picked[:, S : S + H], ds_table[:].indirect(k1_t[:]))
+        nc.vector.tensor_copy(picked_d2[:], ds_table[:].indirect(k2_t[:]))
+        for source, plane in ((picked, planes), (picked_d2, d2_plane)):
+            for q in range(4):
+                queue = nc.sync if (plane is planes and q == 3) else nc.scalar
+                queue.dma_start(plane[32 * q : 32 * q + 4, :].bitcast(I32), source[32 * q : 32 * q + 32 : 8, :].bitcast(I32))
+        nc.sync.dma_start(w_raw[:].bitcast(I32), w1_words[0].bitcast(I32))
+        ws_raw = keep.tile([P, N], U8, name="ws_raw", align_bytes=64)
         for q in range(4):
             rows = w1_scales[0, 4 * q : 4 * q + 4, :].bitcast(I32)
             nc.sync.dma_start(ws_raw[32 * q : 32 * q + 32, :].bitcast(I32), rows.unsqueeze(0).to_broadcast([8, 4, N // 4]))
 
-        d2 = keep.tile([P, H], U32, name="d2", align_bytes=64)
-        xq = [keep.tile([P, HALF], U32, name=f"xq{h}", align_bytes=64) for h in range(2)]
-        nc.vector.tensor_copy(d2[:], d_table[:].bitcast(U32).indirect(k2_t[:]))
-        for h in range(2):
-            nc.vector.tensor_copy(xq[h][:], x_table[:].bitcast(U32).indirect(offs_t[:, 16 * h : 16 * (h + 1)]))
-        d1 = shared.tile([P, H], U32, name="d1", align_bytes=64, offset=0)
+        d1 = keep.tile([P, H], U32, name="d1", align_bytes=64)
+        x_first = keep.tile([P, HALF], U32, name="x_first", align_bytes=64)
         nc.vector.tensor_copy(d1[:], d_table[:].bitcast(U32).indirect(k1_t[:]))
+        nc.vector.tensor_copy(x_first[:], x_table[:].bitcast(U32).indirect(offs_t[:, 0:16]))
+        d2 = shared.tile([P, H], U32, name="d2", align_bytes=64, offset=0)
+        nc.vector.tensor_copy(d2[:], d_table[:].bitcast(U32).indirect(k2_t[:]))
+        x_second = shared.tile([P, HALF], U32, name="x_second", align_bytes=64, offset=2 * H * 4)
+        nc.vector.tensor_copy(x_second[:], x_table[:].bitcast(U32).indirect(offs_t[:, 16:32]))
+        xq = [x_first, x_second]
 
-        w_dealt = shared.tile([P, 2 * N], U8, name="w_dealt", align_bytes=64, offset=4 * H)
-        w_plane = shared.tile([P, N], U8, name="w_plane", align_bytes=64, offset=4 * H + 2 * N)
-        nc.vector.tensor_copy(
+        w_dealt = keep.tile([P, 2 * N], U8, name="w_dealt", align_bytes=64)
+        w_plane = keep.tile([P, N], U8, name="w_plane", align_bytes=64)
+        nc.gpsimd.tensor_copy(
             w_dealt[:].rearrange("p (t m b) -> p t m b", t=4, b=2), w_raw[:].rearrange("p (m t b) -> p t m b", t=4, b=2)
         )
-        nc.vector.tensor_copy(w_plane[:].rearrange("p (t m) -> p t m", t=4), ws_raw[:].rearrange("p (m t) -> p t m", t=4))
+        nc.gpsimd.tensor_copy(w_plane[:].rearrange("p (t m) -> p t m", t=4), ws_raw[:].rearrange("p (m t) -> p t m", t=4))
 
         def score_pass(bank, c, keys, key_scale, start, stop):
             nc.tensor.matmul_mx(
                 out=bank[:],
                 lhsT=xq[c // 2][:, P * (c % 2) : P * (c % 2 + 1)].bitcast(FP8X4),
-                lhsT_scale=planes[:, H + P * c : H + P * (c + 1)],
+                lhsT_scale=planes[:, P * c : P * (c + 1)],
                 rhs=keys[:].bitcast(FP8X4),
                 rhs_scale=key_scale,
                 start=start,
                 stop=stop,
             )
 
-        banks = [psum.tile([P, H], F32, name=f"score{c}", tag=f"score{c}") for c in range(TILES)]
-        fine_bank = psum.tile([P, H], F32, name="fine_bank", tag="fine")
-        fine = keep.tile([P, 4, P], F32, name="fine", align_bytes=64)
-        coarse = keep.tile([P, 4, P], F32, name="coarse", align_bytes=64)
-        for c in range(LAST - 1):
-            score_pass(banks[c], c, d2, planes[:, 0:H], True, False)
-        score_pass(fine_bank, LAST, d2, planes[:, 0:H], True, True)
-        nc.scalar.copy(fine[:], fine_bank[:].rearrange("p (m t) -> p t m", t=4))
-
         y_codes = keep.tile([P, S], I32, name="y_codes", align_bytes=64)
         y_scales = keep.tile([P, S], U8, name="y_scales", align_bytes=64)
         out_rows = out_0.rearrange("(p t) j -> p t j", t=4)
         out_words = out_1[0].rearrange("p j t -> p (j t)").bitcast(I32)
 
-        z_rows = [keep.tile([P, 2, P, 2], BF16, name=f"z_rows{c}", align_bytes=64) for c in range(LAST)]
-        z_cols = [keep.tile([P, P, 4], BF16, name=f"z_cols{c}", align_bytes=64) for c in range(TILES)]
+        z_rows = {}
+        z_cols = {}
         z_codes = [keep.tile([P, P], U32, name=f"z_codes{c}", align_bytes=64) for c in range(TILES)]
         z_scales = [keep.tile([P, P], U8, name=f"z_scales{c}", align_bytes=64) for c in range(TILES)]
         y = [keep.tile([P, 4, P], F32, name=f"y{c}", align_bytes=64) for c in range(TILES)]
-        early_round = keep.tile([P, 2 * P, 4], BF16, name="early_round", align_bytes=64)
-        late_round = [keep.tile([P, P, 4], BF16, name=f"late_round{c}", align_bytes=64) for c in range(2)]
-        y_round = [early_round[:, 0:P], early_round[:, P : 2 * P], late_round[0][:], late_round[1][:]]
+        y_round = [keep.tile([P, 2 * P, 4], BF16, name=f"y_round{h}", align_bytes=64) for h in range(2)]
+        coarse = keep.tile([P, H], F32, name="coarse", align_bytes=64)
+        summed = shared.tile([P, H], F32, name="summed", align_bytes=64, offset=SUM_AT)
+        score_tags = ["b", "d", "e", "f"]
+        turn_tags = ["a", "d", "c", "g"]
+        out_tags = [["b", "h"], ["a"], ["e"], ["c", "d"]]
+        banks = {}
 
-        def score(c):
-            if c == LAST - 1:
-                score_pass(banks[c], c, d2, planes[:, 0:H], True, False)
-            score_pass(banks[c], c, d1, d1_plane[:], False, False)
-            score_pass(banks[c], c, d1, d1_plane[:], False, True)
-            if c == 1:
-                score_pass(banks[LAST], LAST, d1, d1_plane[:], True, True)
-                nc.scalar.activation(coarse[:], banks[LAST][:].rearrange("p (m t) -> p t m", t=4), ACT.Copy, scale=2.0)
+        def coarse_score():
+            bank = psum.tile([P, H], F32, name="coarse_bank", tag="c")
+            score_pass(bank, SUMMED, d1, planes[:, S : S + H], True, True)
+            nc.scalar.activation(coarse[:], bank[:], ACT.Copy, scale=2.0)
 
-        def weigh(c):
+        def open_score(c):
+            banks[c] = psum.tile([P, H], F32, name="score", tag=score_tags[c])
+            if c != SUMMED:
+                score_pass(banks[c], c, d1, planes[:, S : S + H], True, False)
+
+        def close_score(c):
+            if c == SUMMED:
+                score_pass(banks[c], c, d2, d2_plane[:], True, True)
+                nc.vector.tensor_tensor(summed[:], banks[c][:], coarse[:], ALU.add)
+                banks[c] = summed
+                return
+            score_pass(banks[c], c, d2, d2_plane[:], False, False)
+            score_pass(banks[c], c, d1, planes[:, S : S + H], False, True)
+
+        def weigh_and_turn(c):
+            z_rows[c] = keep.tile([P, 2, P, 2], BF16, name=f"z_rows{c}", align_bytes=64)
+            z_cols[c] = keep.tile([P, P, 4], BF16, name=f"z_cols{c}", align_bytes=64)
             view = banks[c][:].rearrange("p (m u e) -> p u m e", u=2, e=2)
             for u in range(2):
                 nc.vector.scalar_tensor_tensor(z_rows[c][:, u], view[:, u], 0.0, g_rows[:, u], ALU.max, ALU.mult)
-
-        def turn(c):
-            turned = psum.tile([P, 2, P], F32, name="turned", tag="turned", bufs=2)
+            turned = psum.tile([P, 2, P], F32, name="turned", tag=turn_tags[c])
             words = z_rows[c][:].rearrange("p u m e -> p (u m e)").bitcast(F32)
             for u in range(2):
                 nc.tensor.transpose(turned[:, u, :], words[:, P * u : P * (u + 1)], ident[:])
@@ -158,38 +167,15 @@ def tile_picked_rpqscore_relu_po_kernel(
                 turned[:].rearrange("p u j -> p j u"),
             )
 
-        summed = psum.tile([P, 4, P], F32, name="summed", tag="fine")
-
-        def turn_last():
-            for t in range(4):
-                nc.tensor.matmul(summed[:, t, :], fine[:, t, :], ident[:], start=True, stop=False, is_transpose=True)
-                nc.tensor.matmul(summed[:, t, :], coarse[:, t, :], ident[:], start=False, stop=True, is_transpose=True)
-
-        def weigh_last():
-            nc.vector.scalar_tensor_tensor(
-                z_cols[LAST][:],
-                summed[:].rearrange("p t j -> p j t"),
-                0.0,
-                g_cols[:].unsqueeze(1).to_broadcast([P, P, 4]),
-                ALU.max,
-                ALU.mult,
-            )
-
-        def quantise_z(c):
+        def values(c):
             nc.vector.quantize_mx(
                 out=z_codes[c][:].bitcast(FP8X4), scales=z_scales[c][:], in_=z_cols[c][:].rearrange("p j t -> p (j t)")
             )
-
-        def values(c):
-            if c < 2:
-                bank = psum.tile([P, 4, P], F32, name="out_bank", tag=f"score{c}")
-                slots = [bank[:, t, :] for t in range(4)]
-            else:
-                pair = [psum.tile([P, 2, P], F32, name="out_pair", tag=tag) for tag in (("score2", "spare") if c == 2 else ("score3", "score0"))]
-                slots = [pair[t // 2][:, t % 2, :] for t in range(4)]
+            each = 4 // len(out_tags[c])
+            parts = [psum.tile([P, each, P], F32, name="out_bank", tag=tag) for tag in out_tags[c]]
             for t in range(4):
                 nc.tensor.matmul_mx(
-                    out=slots[t],
+                    out=parts[t // each][:, t % each, :],
                     lhsT=w_dealt[:, 2 * P * t : 2 * P * (t + 1)].bitcast(FP4X4),
                     lhsT_scale=w_plane[:, P * t : P * (t + 1)],
                     rhs=z_codes[c][:].bitcast(FP8X4),
@@ -197,41 +183,41 @@ def tile_picked_rpqscore_relu_po_kernel(
                     start=True,
                     stop=True,
                 )
-            if c < 2:
-                nc.scalar.copy(y[c][:], bank[:])
-            else:
-                nc.scalar.copy(y[c][:, 0:2], pair[0][:])
-                nc.vector.tensor_copy(y[c][:, 2:4], pair[1][:])
-            nc.sync.dma_start(out_rows[:, :, P * c : P * (c + 1)], y[c][:])
-
-        def round_y(c):
-            nc.vector.tensor_copy(y_round[c], y[c][:].rearrange("p t j -> p j t"))
-
-        def quantise_y(c):
+            cols = slice(P * c, P * (c + 1))
             if c == 0:
+                for h in range(2):
+                    nc.scalar.copy(y[c][:, 2 * h : 2 * h + 2], parts[h][:])
+                    nc.sync.dma_start(out_rows[:, 2 * h : 2 * h + 2, cols], y[c][:, 2 * h : 2 * h + 2])
                 return
-            cols = slice(0, 2 * P) if c == 1 else slice(P * c, P * (c + 1))
-            rounded = early_round[:] if c == 1 else y_round[c]
-            nc.vector.quantize_mx(
-                out=y_codes[:, cols].bitcast(FP8X4), scales=y_scales[:, cols], in_=rounded.rearrange("p j t -> p (j t)")
-            )
-            if c >= TILES - 2:
-                done = slice(0, P * (c + 1)) if c == TILES - 2 else cols
-                nc.sync.dma_start(out_words[:, done], y_codes[:, done])
+            if c == 1:
+                nc.vector.tensor_copy(y[c][:], parts[0][:])
+            else:
+                nc.scalar.copy(y[c][:, 0:each], parts[0][:])
+            if each < 4:
+                nc.vector.tensor_copy(y[c][:, each:4], parts[1][:])
+            nc.sync.dma_start(out_rows[:, :, cols], y[c][:])
 
-        for c in range(LAST):
-            score(c)
-        for c in range(LAST):
-            weigh(c)
-            turn(c)
-            if c == 0:
-                turn_last()
-        weigh_last()
-        stages = [quantise_z, values, round_y, quantise_y]
-        for step in range(TILES + len(stages) - 1):
-            for s in reversed(range(len(stages))):
-                if 0 <= step - s < TILES:
-                    stages[s](step - s)
+        def planes_out(c):
+            copy = [nc.gpsimd.tensor_copy, nc.vector.tensor_copy, nc.scalar.copy, nc.vector.tensor_copy][c]
+            copy(y_round[c // 2][:, P * (c % 2) : P * (c % 2 + 1)], y[c][:].rearrange("p t j -> p j t"))
+            if c % 2 == 1:
+                cols = slice(P * (c - 1), P * (c + 1))
+                nc.vector.quantize_mx(
+                    out=y_codes[:, cols].bitcast(FP8X4), scales=y_scales[:, cols], in_=y_round[c // 2][:].rearrange("p j t -> p (j t)")
+                )
+                nc.sync.dma_start(out_words[:, cols], y_codes[:, cols])
+
+        coarse_score()
+        for c in range(2):
+            open_score(c)
+        for c in range(2):
+            close_score(c)
+        for c in range(2, TILES):
+            open_score(c)
+            close_score(c)
+        for stage in (weigh_and_turn, values, planes_out):
+            for c in range(TILES):
+                stage(c)
 
         for q in range(4):
             queue = nc.scalar if q % 2 == 0 else nc.sync

@@ -21,9 +21,7 @@ P = 128
 TILES = S // P
 LAST = TILES - 1
 HALF = S // 2
-SUMMED = 0
-Z_AT = 2 * H * 4 + 4 * G
-SUM_AT = Z_AT + 2 * H
+SUMMED = 1
 
 
 def tile_picked_rpqscore_relu_po_kernel(
@@ -39,10 +37,10 @@ def tile_picked_rpqscore_relu_po_kernel(
         k1_t = keep.tile([P, H // 16], U16, name="k1_t")
         k2_t = keep.tile([P, H // 16], U16, name="k2_t")
         x_table = keep.tile([P, T], I32, name="x_table", align_bytes=64)
-        d_table = shared.tile([P, G], I32, name="d_table", align_bytes=64, offset=2 * H * 4)
+        d_table = shared.tile([P, G], I32, name="d_table", align_bytes=64, offset=0)
         xs_table = keep.tile([P, T], U8, name="xs_table", align_bytes=64)
         ds_table = keep.tile([P, G], U8, name="ds_table", align_bytes=64)
-        picked = shared.tile([P, S + H], U8, name="picked", align_bytes=64, offset=0)
+        picked = keep.tile([P, S + H], U8, name="picked", align_bytes=64)
         planes = keep.tile([P, S + H], U8, name="planes", align_bytes=64)
         picked_d2 = keep.tile([P, H], U8, name="picked_d2", align_bytes=64)
         d2_plane = keep.tile([P, H], U8, name="d2_plane", align_bytes=64)
@@ -51,7 +49,6 @@ def tile_picked_rpqscore_relu_po_kernel(
         g_rows = keep.tile([P, 2, P, 2], F32, name="g_rows", align_bytes=64)
         ident = keep.tile([P, P], F32, name="ident")
 
-        nc.vector.memset(xs_table[:].bitcast(I32), 0)
         nc.vector.memset(ds_table[:, 0 : G // 2].bitcast(I32), 0)
         nc.gpsimd.memset(ds_table[:, G // 2 : G].bitcast(I32), 0)
         nc.vector.memset(planes[:].bitcast(I32), 0)
@@ -60,12 +57,12 @@ def tile_picked_rpqscore_relu_po_kernel(
 
         nc.sync.dma_start(offs_t[:], offs)
         nc.sync.dma_start(g_raw[:], gn.rearrange("(p t) o -> p (t o)", t=4))
-        nc.sync.dma_start(xs_table[0:P:8, :].bitcast(I32), x_scales[0].bitcast(I32))
+        nc.sync.dma_start(xs_table[:].bitcast(I32), x_scales[0].bitcast(I32).unsqueeze(1).to_broadcast([16, 8, T // 4]))
         nc.sync.dma_start(k1_t[:], k1)
         nc.sync.dma_start(ds_table[0:P:8, :].bitcast(I32), d_scales[0].bitcast(I32))
         nc.sync.dma_start(k2_t[:], k2)
-        nc.sync.dma_start(d_table[:], d_words[0].rearrange("p n t -> p (n t)").bitcast(I32))
         nc.sync.dma_start(x_table[:], x_words[0].rearrange("p n t -> p (n t)").bitcast(I32))
+        nc.sync.dma_start(d_table[:], d_words[0].rearrange("p n t -> p (n t)").bitcast(I32))
 
         g_scaled = keep.tile([P, 4], F32, name="g_scaled")
         nc.scalar.activation(g_scaled[:], g_raw[:], ACT.Copy, scale=0.03125)
@@ -79,7 +76,7 @@ def tile_picked_rpqscore_relu_po_kernel(
         nc.vector.tensor_copy(picked_d2[:], ds_table[:].indirect(k2_t[:]))
         for source, plane in ((picked, planes), (picked_d2, d2_plane)):
             for q in range(4):
-                queue = nc.sync if (plane is planes and q == 3) else nc.scalar
+                queue = nc.sync if (plane is d2_plane and q >= 2) else nc.scalar
                 queue.dma_start(plane[32 * q : 32 * q + 4, :].bitcast(I32), source[32 * q : 32 * q + 32 : 8, :].bitcast(I32))
         nc.sync.dma_start(w_raw[:].bitcast(I32), w1_words[0].bitcast(I32))
         ws_raw = keep.tile([P, N], U8, name="ws_raw", align_bytes=64)
@@ -87,13 +84,14 @@ def tile_picked_rpqscore_relu_po_kernel(
             rows = w1_scales[0, 4 * q : 4 * q + 4, :].bitcast(I32)
             nc.sync.dma_start(ws_raw[32 * q : 32 * q + 32, :].bitcast(I32), rows.unsqueeze(0).to_broadcast([8, 4, N // 4]))
 
-        d1 = keep.tile([P, H], U32, name="d1", align_bytes=64)
+        d1 = [keep.tile([P, HALF], U32, name=f"d1_{h}", align_bytes=64) for h in range(2)]
         x_first = keep.tile([P, HALF], U32, name="x_first", align_bytes=64)
-        nc.vector.tensor_copy(d1[:], d_table[:].bitcast(U32).indirect(k1_t[:]))
+        d2 = keep.tile([P, H], U32, name="d2", align_bytes=64)
         nc.vector.tensor_copy(x_first[:], x_table[:].bitcast(U32).indirect(offs_t[:, 0:16]))
-        d2 = shared.tile([P, H], U32, name="d2", align_bytes=64, offset=0)
+        for h in range(2):
+            nc.vector.tensor_copy(d1[h][:], d_table[:].bitcast(U32).indirect(k1_t[:, 16 * h : 16 * (h + 1)]))
         nc.vector.tensor_copy(d2[:], d_table[:].bitcast(U32).indirect(k2_t[:]))
-        x_second = shared.tile([P, HALF], U32, name="x_second", align_bytes=64, offset=2 * H * 4)
+        x_second = shared.tile([P, HALF], U32, name="x_second", align_bytes=64, offset=0)
         nc.vector.tensor_copy(x_second[:], x_table[:].bitcast(U32).indirect(offs_t[:, 16:32]))
         xq = [x_first, x_second]
 
@@ -104,16 +102,23 @@ def tile_picked_rpqscore_relu_po_kernel(
         )
         nc.gpsimd.tensor_copy(w_plane[:].rearrange("p (t m) -> p t m", t=4), ws_raw[:].rearrange("p (m t) -> p t m", t=4))
 
-        def score_pass(bank, c, keys, key_scale, start, stop):
+        def score_pass(out, c, keys, key_scale, start, stop):
             nc.tensor.matmul_mx(
-                out=bank[:],
+                out=out,
                 lhsT=xq[c // 2][:, P * (c % 2) : P * (c % 2 + 1)].bitcast(FP8X4),
                 lhsT_scale=planes[:, P * c : P * (c + 1)],
-                rhs=keys[:].bitcast(FP8X4),
+                rhs=keys.bitcast(FP8X4),
                 rhs_scale=key_scale,
                 start=start,
                 stop=stop,
             )
+
+        def d1_pass(bank, c, h, start, stop):
+            first = S + HALF * h
+            score_pass(bank[:, HALF * h : HALF * (h + 1)], c, d1[h][:], planes[:, first : first + HALF], start, stop)
+
+        def d2_pass(bank, c, start):
+            score_pass(bank[:], c, d2[:], d2_plane[:], start, True)
 
         y_codes = keep.tile([P, S], I32, name="y_codes", align_bytes=64)
         y_scales = keep.tile([P, S], U8, name="y_scales", align_bytes=64)
@@ -127,30 +132,32 @@ def tile_picked_rpqscore_relu_po_kernel(
         y = [keep.tile([P, 4, P], F32, name=f"y{c}", align_bytes=64) for c in range(TILES)]
         y_round = [keep.tile([P, 2 * P, 4], BF16, name=f"y_round{h}", align_bytes=64) for h in range(2)]
         coarse = keep.tile([P, H], F32, name="coarse", align_bytes=64)
-        summed = shared.tile([P, H], F32, name="summed", align_bytes=64, offset=SUM_AT)
-        score_tags = ["b", "d", "e", "f"]
-        turn_tags = ["a", "d", "c", "g"]
-        out_tags = [["b", "h"], ["a"], ["e"], ["c", "d"]]
+        summed = keep.tile([P, H], F32, name="summed", align_bytes=64)
+        score_tags = ["b", "d", "c", "d"]
+        turn_tags = ["a", "e", "f", "g"]
+        out_tags = [["b", "h"], ["a"], ["c"], ["d", "e"]]
         banks = {}
 
-        def coarse_score():
-            bank = psum.tile([P, H], F32, name="coarse_bank", tag="c")
-            score_pass(bank, SUMMED, d1, planes[:, S : S + H], True, True)
-            nc.scalar.activation(coarse[:], bank[:], ACT.Copy, scale=2.0)
+        def first_scores():
+            coarse_bank = psum.tile([P, H], F32, name="coarse_bank", tag="c")
+            fine_bank = psum.tile([P, H], F32, name="fine_bank", tag=score_tags[SUMMED])
+            banks[0] = psum.tile([P, H], F32, name="score", tag=score_tags[0])
+            for h in range(2):
+                d1_pass(coarse_bank, SUMMED, h, True, True)
+                d1_pass(banks[0], 0, h, h == 0, False)
+                d1_pass(banks[0], 0, h, False, False)
+            nc.scalar.activation(coarse[:], coarse_bank[:], ACT.Copy, scale=2.0)
+            d2_pass(fine_bank, SUMMED, True)
+            nc.vector.tensor_tensor(summed[:], fine_bank[:], coarse[:], ALU.add)
+            banks[SUMMED] = summed
+            d2_pass(banks[0], 0, False)
 
-        def open_score(c):
+        def score(c):
             banks[c] = psum.tile([P, H], F32, name="score", tag=score_tags[c])
-            if c != SUMMED:
-                score_pass(banks[c], c, d1, planes[:, S : S + H], True, False)
-
-        def close_score(c):
-            if c == SUMMED:
-                score_pass(banks[c], c, d2, d2_plane[:], True, True)
-                nc.vector.tensor_tensor(summed[:], banks[c][:], coarse[:], ALU.add)
-                banks[c] = summed
-                return
-            score_pass(banks[c], c, d2, d2_plane[:], False, False)
-            score_pass(banks[c], c, d1, planes[:, S : S + H], False, True)
+            for h in range(2):
+                d1_pass(banks[c], c, h, h == 0, False)
+                d1_pass(banks[c], c, h, False, False)
+            d2_pass(banks[c], c, False)
 
         def weigh_and_turn(c):
             z_rows[c] = keep.tile([P, 2, P, 2], BF16, name=f"z_rows{c}", align_bytes=64)
@@ -207,14 +214,9 @@ def tile_picked_rpqscore_relu_po_kernel(
                 )
                 nc.sync.dma_start(out_words[:, cols], y_codes[:, cols])
 
-        coarse_score()
-        for c in range(2):
-            open_score(c)
-        for c in range(2):
-            close_score(c)
+        first_scores()
         for c in range(2, TILES):
-            open_score(c)
-            close_score(c)
+            score(c)
         for stage in (weigh_and_turn, values, planes_out):
             for c in range(TILES):
                 stage(c)

@@ -22,6 +22,7 @@ TILES = S // P
 LAST = TILES - 1
 HALF = S // 2
 SUMMED = 1
+ZERO_SPLIT = 3 * G // 4
 
 
 def tile_picked_rpqscore_relu_po_kernel(
@@ -49,18 +50,18 @@ def tile_picked_rpqscore_relu_po_kernel(
         g_rows = keep.tile([P, 2, P, 2], F32, name="g_rows", align_bytes=64)
         ident = keep.tile([P, P], F32, name="ident")
 
-        nc.vector.memset(ds_table[:, 0 : G // 2].bitcast(I32), 0)
-        nc.gpsimd.memset(ds_table[:, G // 2 : G].bitcast(I32), 0)
+        nc.vector.memset(ds_table[:, 0:ZERO_SPLIT].bitcast(I32), 0)
+        nc.gpsimd.memset(ds_table[:, ZERO_SPLIT:G].bitcast(I32), 0)
         nc.vector.memset(planes[:].bitcast(I32), 0)
         nc.vector.memset(d2_plane[:].bitcast(I32), 0)
         make_identity(nc, ident[:])
 
+        nc.sync.dma_start(xs_table[:].bitcast(I32), x_scales[0].bitcast(I32).unsqueeze(1).to_broadcast([16, 8, T // 4]))
         nc.sync.dma_start(offs_t[:], offs)
         nc.sync.dma_start(g_raw[:], gn.rearrange("(p t) o -> p (t o)", t=4))
-        nc.sync.dma_start(xs_table[:].bitcast(I32), x_scales[0].bitcast(I32).unsqueeze(1).to_broadcast([16, 8, T // 4]))
         nc.sync.dma_start(k1_t[:], k1)
-        nc.sync.dma_start(ds_table[0:P:8, :].bitcast(I32), d_scales[0].bitcast(I32))
         nc.sync.dma_start(k2_t[:], k2)
+        nc.sync.dma_start(ds_table[0:P:8, :].bitcast(I32), d_scales[0].bitcast(I32))
         nc.sync.dma_start(x_table[:], x_words[0].rearrange("p n t -> p (n t)").bitcast(I32))
         nc.sync.dma_start(d_table[:], d_words[0].rearrange("p n t -> p (n t)").bitcast(I32))
 
@@ -129,7 +130,9 @@ def tile_picked_rpqscore_relu_po_kernel(
         z_cols = {}
         z_codes = [keep.tile([P, P], U32, name=f"z_codes{c}", align_bytes=64) for c in range(TILES)]
         z_scales = [keep.tile([P, P], U8, name=f"z_scales{c}", align_bytes=64) for c in range(TILES)]
-        y = [keep.tile([P, 4, P], F32, name=f"y{c}", align_bytes=64) for c in range(TILES)]
+        y_late = keep.tile([P, 4, HALF], F32, name="y_late", align_bytes=64)
+        y = [keep.tile([P, 4, P], F32, name=f"y{c}", align_bytes=64) for c in range(2)]
+        y = y + [y_late[:, :, 0:P], y_late[:, :, P:HALF]]
         y_round = [keep.tile([P, 2 * P, 4], BF16, name=f"y_round{h}", align_bytes=64) for h in range(2)]
         coarse = keep.tile([P, H], F32, name="coarse", align_bytes=64)
         summed = keep.tile([P, H], F32, name="summed", align_bytes=64)
@@ -202,7 +205,10 @@ def tile_picked_rpqscore_relu_po_kernel(
                 nc.scalar.copy(y[c][:, 0:each], parts[0][:])
             if each < 4:
                 nc.vector.tensor_copy(y[c][:, each:4], parts[1][:])
-            nc.sync.dma_start(out_rows[:, :, cols], y[c][:])
+            if c == 1:
+                nc.sync.dma_start(out_rows[:, :, cols], y[c][:])
+            if c == LAST:
+                nc.sync.dma_start(out_rows[:, :, HALF:S], y_late[:])
 
         def planes_out(c):
             copy = [nc.gpsimd.tensor_copy, nc.vector.tensor_copy, nc.scalar.copy, nc.vector.tensor_copy][c]
@@ -212,7 +218,6 @@ def tile_picked_rpqscore_relu_po_kernel(
                 nc.vector.quantize_mx(
                     out=y_codes[:, cols].bitcast(FP8X4), scales=y_scales[:, cols], in_=y_round[c // 2][:].rearrange("p j t -> p (j t)")
                 )
-                nc.sync.dma_start(out_words[:, cols], y_codes[:, cols])
 
         first_scores()
         for c in range(2, TILES):
@@ -221,6 +226,7 @@ def tile_picked_rpqscore_relu_po_kernel(
             for c in range(TILES):
                 stage(c)
 
+        nc.sync.dma_start(out_words, y_codes[:])
         for q in range(4):
             queue = nc.scalar if q % 2 == 0 else nc.sync
             queue.dma_start(out_2[0, 4 * q : 4 * q + 4, :].bitcast(I32), y_scales[32 * q : 32 * q + 4, :].bitcast(I32))

@@ -31,14 +31,13 @@ def tile_picked_rpqscore_relu_po_kernel(
     nc = tc.nc
     with ExitStack() as ctx:
         keep = ctx.enter_context(tc.tile_pool(name="keep", bufs=1))
-        shared = ctx.enter_context(tc.tile_pool(name="shared", bufs=1))
         psum = ctx.enter_context(tc.psum_pool(name="psum", bufs=1))
 
         offs_t = keep.tile([P, S // 16], U16, name="offs_t")
         k1_t = keep.tile([P, H // 16], U16, name="k1_t")
         k2_t = keep.tile([P, H // 16], U16, name="k2_t")
         x_table = keep.tile([P, T], I32, name="x_table", align_bytes=64)
-        d_table = shared.tile([P, G], I32, name="d_table", align_bytes=64, offset=0)
+        d_table = keep.tile([P, G], I32, name="d_table", align_bytes=64)
         xs_table = keep.tile([P, T], U8, name="xs_table", align_bytes=64)
         ds_table = keep.tile([P, G], U8, name="ds_table", align_bytes=64)
         picked = keep.tile([P, S + H], U8, name="picked", align_bytes=64)
@@ -60,8 +59,8 @@ def tile_picked_rpqscore_relu_po_kernel(
         nc.sync.dma_start(offs_t[:], offs)
         nc.sync.dma_start(g_raw[:], gn.rearrange("(p t) o -> p (t o)", t=4))
         nc.sync.dma_start(k1_t[:], k1)
-        nc.sync.dma_start(k2_t[:], k2)
         nc.sync.dma_start(ds_table[0:P:8, :].bitcast(I32), d_scales[0].bitcast(I32))
+        nc.sync.dma_start(k2_t[:], k2)
         nc.sync.dma_start(x_table[:], x_words[0].rearrange("p n t -> p (n t)").bitcast(I32))
         nc.sync.dma_start(d_table[:], d_words[0].rearrange("p n t -> p (n t)").bitcast(I32))
 
@@ -77,7 +76,7 @@ def tile_picked_rpqscore_relu_po_kernel(
         nc.vector.tensor_copy(picked_d2[:], ds_table[:].indirect(k2_t[:]))
         for source, plane in ((picked, planes), (picked_d2, d2_plane)):
             for q in range(4):
-                queue = nc.sync if (plane is d2_plane and q >= 2) else nc.scalar
+                queue = nc.scalar if plane is planes else [nc.gpsimd, nc.scalar, nc.sync, nc.scalar][q]
                 queue.dma_start(plane[32 * q : 32 * q + 4, :].bitcast(I32), source[32 * q : 32 * q + 32 : 8, :].bitcast(I32))
         nc.sync.dma_start(w_raw[:].bitcast(I32), w1_words[0].bitcast(I32))
         ws_raw = keep.tile([P, N], U8, name="ws_raw", align_bytes=64)
@@ -85,16 +84,12 @@ def tile_picked_rpqscore_relu_po_kernel(
             rows = w1_scales[0, 4 * q : 4 * q + 4, :].bitcast(I32)
             nc.sync.dma_start(ws_raw[32 * q : 32 * q + 32, :].bitcast(I32), rows.unsqueeze(0).to_broadcast([8, 4, N // 4]))
 
-        d1 = [keep.tile([P, HALF], U32, name=f"d1_{h}", align_bytes=64) for h in range(2)]
-        x_first = keep.tile([P, HALF], U32, name="x_first", align_bytes=64)
-        d2 = keep.tile([P, H], U32, name="d2", align_bytes=64)
-        nc.vector.tensor_copy(x_first[:], x_table[:].bitcast(U32).indirect(offs_t[:, 0:16]))
-        for h in range(2):
-            nc.vector.tensor_copy(d1[h][:], d_table[:].bitcast(U32).indirect(k1_t[:, 16 * h : 16 * (h + 1)]))
-        nc.vector.tensor_copy(d2[:], d_table[:].bitcast(U32).indirect(k2_t[:]))
-        x_second = shared.tile([P, HALF], U32, name="x_second", align_bytes=64, offset=0)
-        nc.vector.tensor_copy(x_second[:], x_table[:].bitcast(U32).indirect(offs_t[:, 16:32]))
-        xq = [x_first, x_second]
+        xq = keep.tile([P, S], U32, name="xq", align_bytes=64)
+        nc.vector.tensor_copy(xq[:], x_table[:].bitcast(U32).indirect(offs_t[:]))
+        keys = [[keep.tile([P, HALF], U32, name=f"keys{v}_{h}", align_bytes=64) for h in range(2)] for v in range(2)]
+        for v, picks in enumerate((k1_t, k2_t)):
+            for h in range(2):
+                nc.vector.tensor_copy(keys[v][h][:], d_table[:].bitcast(U32).indirect(picks[:, 16 * h : 16 * (h + 1)]))
 
         w_dealt = keep.tile([P, 2 * N], U8, name="w_dealt", align_bytes=64)
         w_plane = keep.tile([P, N], U8, name="w_plane", align_bytes=64)
@@ -103,23 +98,17 @@ def tile_picked_rpqscore_relu_po_kernel(
         )
         nc.gpsimd.tensor_copy(w_plane[:].rearrange("p (t m) -> p t m", t=4), ws_raw[:].rearrange("p (m t) -> p t m", t=4))
 
-        def score_pass(out, c, keys, key_scale, start, stop):
+        def score_pass(out, c, v, h, start, stop):
+            key_plane = [planes[:, S : S + H], d2_plane[:]][v]
             nc.tensor.matmul_mx(
                 out=out,
-                lhsT=xq[c // 2][:, P * (c % 2) : P * (c % 2 + 1)].bitcast(FP8X4),
+                lhsT=xq[:, P * c : P * (c + 1)].bitcast(FP8X4),
                 lhsT_scale=planes[:, P * c : P * (c + 1)],
-                rhs=keys.bitcast(FP8X4),
-                rhs_scale=key_scale,
+                rhs=keys[v][h][:].bitcast(FP8X4),
+                rhs_scale=key_plane[:, HALF * h : HALF * (h + 1)],
                 start=start,
                 stop=stop,
             )
-
-        def d1_pass(bank, c, h, start, stop):
-            first = S + HALF * h
-            score_pass(bank[:, HALF * h : HALF * (h + 1)], c, d1[h][:], planes[:, first : first + HALF], start, stop)
-
-        def d2_pass(bank, c, start):
-            score_pass(bank[:], c, d2[:], d2_plane[:], start, True)
 
         y_codes = keep.tile([P, S], I32, name="y_codes", align_bytes=64)
         y_scales = keep.tile([P, S], U8, name="y_scales", align_bytes=64)
@@ -136,38 +125,56 @@ def tile_picked_rpqscore_relu_po_kernel(
         y_round = [keep.tile([P, 2 * P, 4], BF16, name=f"y_round{h}", align_bytes=64) for h in range(2)]
         coarse = keep.tile([P, H], F32, name="coarse", align_bytes=64)
         summed = keep.tile([P, H], F32, name="summed", align_bytes=64)
-        score_tags = ["b", "d", "c", "d"]
-        turn_tags = ["a", "e", "f", "g"]
-        out_tags = [["b", "h"], ["a"], ["c"], ["d", "e"]]
-        banks = {}
-
-        def first_scores():
-            coarse_bank = psum.tile([P, H], F32, name="coarse_bank", tag="c")
-            fine_bank = psum.tile([P, H], F32, name="fine_bank", tag=score_tags[SUMMED])
-            banks[0] = psum.tile([P, H], F32, name="score", tag=score_tags[0])
-            for h in range(2):
-                d1_pass(coarse_bank, SUMMED, h, True, True)
-                d1_pass(banks[0], 0, h, h == 0, False)
-                d1_pass(banks[0], 0, h, False, False)
-            nc.scalar.activation(coarse[:], coarse_bank[:], ACT.Copy, scale=2.0)
-            d2_pass(fine_bank, SUMMED, True)
-            nc.vector.tensor_tensor(summed[:], fine_bank[:], coarse[:], ALU.add)
-            banks[SUMMED] = summed
-            d2_pass(banks[0], 0, False)
-
-        def score(c):
-            banks[c] = psum.tile([P, H], F32, name="score", tag=score_tags[c])
-            for h in range(2):
-                d1_pass(banks[c], c, h, h == 0, False)
-                d1_pass(banks[c], c, h, False, False)
-            d2_pass(banks[c], c, False)
-
-        def weigh_and_turn(c):
+        turn_tags = ["g", "h", "a", "e"]
+        out_tags = [["b", "f"], ["g"], ["h"], ["c", "a"]]
+        for c in range(TILES):
             z_rows[c] = keep.tile([P, 2, P, 2], BF16, name=f"z_rows{c}", align_bytes=64)
             z_cols[c] = keep.tile([P, P, 4], BF16, name=f"z_cols{c}", align_bytes=64)
-            view = banks[c][:].rearrange("p (m u e) -> p u m e", u=2, e=2)
+
+        def weigh(c, scores, first, count):
+            view = scores.rearrange("p (m u e) -> p u m e", u=2, e=2)
             for u in range(2):
-                nc.vector.scalar_tensor_tensor(z_rows[c][:, u], view[:, u], 0.0, g_rows[:, u], ALU.max, ALU.mult)
+                span = slice(first, first + count)
+                nc.vector.scalar_tensor_tensor(z_rows[c][:, u, span], view[:, u], 0.0, g_rows[:, u, span], ALU.max, ALU.mult)
+
+        def first_scores():
+            whole = [psum.tile([P, HALF], F32, name="whole", tag=tag) for tag in ("a", "b")]
+            coarse_bank = [psum.tile([P, HALF], F32, name="coarse_bank", tag=tag) for tag in ("c", "d")]
+            fine_bank = [psum.tile([P, HALF], F32, name="fine_bank", tag=tag) for tag in ("e", "f")]
+            halves = [slice(0, HALF), slice(HALF, H)]
+
+            def coarse_pass(h):
+                score_pass(coarse_bank[h][:], SUMMED, 0, h, True, True)
+                nc.scalar.activation(coarse[:, halves[h]], coarse_bank[h][:], ACT.Copy, scale=2.0)
+
+            def fine_passes(h):
+                score_pass(whole[h][:], 0, 1, h, False, True)
+                score_pass(fine_bank[h][:], SUMMED, 1, h, True, True)
+
+            for h in range(2):
+                score_pass(whole[h][:], 0, 0, h, True, False)
+                score_pass(whole[h][:], 0, 0, h, False, False)
+                if h == 0:
+                    coarse_pass(0)
+            fine_passes(0)
+            coarse_pass(1)
+            fine_passes(1)
+            weigh(0, whole[0][:], 0, P // 2)
+            nc.vector.tensor_tensor(summed[:, halves[0]], fine_bank[0][:], coarse[:, halves[0]], ALU.add)
+            weigh(0, whole[1][:], P // 2, P // 2)
+            weigh(SUMMED, summed[:, halves[0]], 0, P // 2)
+            nc.vector.tensor_tensor(summed[:, halves[1]], fine_bank[1][:], coarse[:, halves[1]], ALU.add)
+            weigh(SUMMED, summed[:, halves[1]], P // 2, P // 2)
+
+        def score(c):
+            bank = psum.tile([P, H], F32, name="score", tag=["c", "d"][c - 2])
+            for v, again in ((0, 2), (1, 1)):
+                for h in range(2):
+                    for n in range(again):
+                        score_pass(bank[:, HALF * h : HALF * (h + 1)], c, v, h, (v, h, n) == (0, 0, 0), (v, h) == (1, 1))
+            return bank
+
+        def turn(c):
             turned = psum.tile([P, 2, P], F32, name="turned", tag=turn_tags[c])
             words = z_rows[c][:].rearrange("p u m e -> p (u m e)").bitcast(F32)
             for u in range(2):
@@ -219,10 +226,16 @@ def tile_picked_rpqscore_relu_po_kernel(
                     out=y_codes[:, cols].bitcast(FP8X4), scales=y_scales[:, cols], in_=y_round[c // 2][:].rearrange("p j t -> p (j t)")
                 )
 
+        late = {}
         first_scores()
         for c in range(2, TILES):
-            score(c)
-        for stage in (weigh_and_turn, values, planes_out):
+            late[c] = score(c)
+        turn(0)
+        turn(SUMMED)
+        for c in range(2, TILES):
+            weigh(c, late[c][:], 0, P)
+            turn(c)
+        for stage in (values, planes_out):
             for c in range(TILES):
                 stage(c)
 

@@ -21,7 +21,8 @@ P = 128
 TILES = S // P
 LAST = TILES - 1
 HALF = S // 2
-SUMMED = 1
+SUMMED = 0
+ASIDE = 1
 ZERO_SPLIT = 3 * G // 4
 
 
@@ -59,8 +60,8 @@ def tile_picked_rpqscore_relu_po_kernel(
         nc.sync.dma_start(offs_t[:], offs)
         nc.sync.dma_start(g_raw[:], gn.rearrange("(p t) o -> p (t o)", t=4))
         nc.sync.dma_start(k1_t[:], k1)
-        nc.sync.dma_start(ds_table[0:P:8, :].bitcast(I32), d_scales[0].bitcast(I32))
         nc.sync.dma_start(k2_t[:], k2)
+        nc.sync.dma_start(ds_table[0:P:8, :].bitcast(I32), d_scales[0].bitcast(I32))
         nc.sync.dma_start(x_table[:], x_words[0].rearrange("p n t -> p (n t)").bitcast(I32))
         nc.sync.dma_start(d_table[:], d_words[0].rearrange("p n t -> p (n t)").bitcast(I32))
 
@@ -76,13 +77,14 @@ def tile_picked_rpqscore_relu_po_kernel(
         nc.vector.tensor_copy(picked_d2[:], ds_table[:].indirect(k2_t[:]))
         for source, plane in ((picked, planes), (picked_d2, d2_plane)):
             for q in range(4):
-                queue = nc.scalar if plane is planes else [nc.gpsimd, nc.scalar, nc.sync, nc.scalar][q]
+                queue = nc.sync if (plane is d2_plane and q >= 2) else nc.scalar
                 queue.dma_start(plane[32 * q : 32 * q + 4, :].bitcast(I32), source[32 * q : 32 * q + 32 : 8, :].bitcast(I32))
-        nc.sync.dma_start(w_raw[:].bitcast(I32), w1_words[0].bitcast(I32))
         ws_raw = keep.tile([P, N], U8, name="ws_raw", align_bytes=64)
         for q in range(4):
             rows = w1_scales[0, 4 * q : 4 * q + 4, :].bitcast(I32)
             nc.sync.dma_start(ws_raw[32 * q : 32 * q + 32, :].bitcast(I32), rows.unsqueeze(0).to_broadcast([8, 4, N // 4]))
+            if q == 0:
+                nc.sync.dma_start(w_raw[:].bitcast(I32), w1_words[0].bitcast(I32))
 
         xq = keep.tile([P, S], U32, name="xq", align_bytes=64)
         nc.vector.tensor_copy(xq[:], x_table[:].bitcast(U32).indirect(offs_t[:]))
@@ -93,10 +95,6 @@ def tile_picked_rpqscore_relu_po_kernel(
 
         w_dealt = keep.tile([P, 2 * N], U8, name="w_dealt", align_bytes=64)
         w_plane = keep.tile([P, N], U8, name="w_plane", align_bytes=64)
-        nc.gpsimd.tensor_copy(
-            w_dealt[:].rearrange("p (t m b) -> p t m b", t=4, b=2), w_raw[:].rearrange("p (m t b) -> p t m b", t=4, b=2)
-        )
-        nc.gpsimd.tensor_copy(w_plane[:].rearrange("p (t m) -> p t m", t=4), ws_raw[:].rearrange("p (m t) -> p t m", t=4))
 
         def score_pass(out, c, v, h, start, stop):
             key_plane = [planes[:, S : S + H], d2_plane[:]][v]
@@ -125,46 +123,51 @@ def tile_picked_rpqscore_relu_po_kernel(
         y_round = [keep.tile([P, 2 * P, 4], BF16, name=f"y_round{h}", align_bytes=64) for h in range(2)]
         coarse = keep.tile([P, H], F32, name="coarse", align_bytes=64)
         summed = keep.tile([P, H], F32, name="summed", align_bytes=64)
-        turn_tags = ["g", "h", "a", "e"]
-        out_tags = [["b", "f"], ["g"], ["h"], ["c", "a"]]
+        turn_tags = ["g", "e", "h", "f"]
+        out_tags = [["b", "a"], ["g"], ["e"], ["c", "h"]]
         for c in range(TILES):
             z_rows[c] = keep.tile([P, 2, P, 2], BF16, name=f"z_rows{c}", align_bytes=64)
             z_cols[c] = keep.tile([P, P, 4], BF16, name=f"z_cols{c}", align_bytes=64)
 
-        def weigh(c, scores, first, count):
+        g_held = g_bank[:].rearrange("p (u e) m -> p u m e", e=2)
+
+        def weigh(c, scores, weights, first, count):
             view = scores.rearrange("p (m u e) -> p u m e", u=2, e=2)
             for u in range(2):
                 span = slice(first, first + count)
-                nc.vector.scalar_tensor_tensor(z_rows[c][:, u, span], view[:, u], 0.0, g_rows[:, u, span], ALU.max, ALU.mult)
+                nc.vector.scalar_tensor_tensor(z_rows[c][:, u, span], view[:, u], 0.0, weights[:, u, span], ALU.max, ALU.mult)
 
         def first_scores():
-            whole = [psum.tile([P, HALF], F32, name="whole", tag=tag) for tag in ("a", "b")]
+            whole = [psum.tile([P, HALF], F32, name="whole", tag=tag) for tag in ("h", "b")]
             coarse_bank = [psum.tile([P, HALF], F32, name="coarse_bank", tag=tag) for tag in ("c", "d")]
             fine_bank = [psum.tile([P, HALF], F32, name="fine_bank", tag=tag) for tag in ("e", "f")]
             halves = [slice(0, HALF), slice(HALF, H)]
+            spans = [slice(0, P // 2), slice(P // 2, P)]
+            kept = keep.tile([P, 2, 2, P // 2, 2], F32, name="kept", align_bytes=64)
 
             def coarse_pass(h):
                 score_pass(coarse_bank[h][:], SUMMED, 0, h, True, True)
                 nc.scalar.activation(coarse[:, halves[h]], coarse_bank[h][:], ACT.Copy, scale=2.0)
 
-            def fine_passes(h):
-                score_pass(whole[h][:], 0, 1, h, False, True)
-                score_pass(fine_bank[h][:], SUMMED, 1, h, True, True)
+            def aside_pass(h):
+                score_pass(whole[h][:], ASIDE, 1, h, False, True)
+                nc.scalar.activation(kept[:, h], whole[h][:].rearrange("p (m u e) -> p u m e", u=2, e=2), ACT.Relu)
+                nc.gpsimd.tensor_tensor(z_rows[ASIDE][:, :, spans[h]], kept[:, h], g_rows[:, :, spans[h]], ALU.mult)
 
-            for h in range(2):
-                score_pass(whole[h][:], 0, 0, h, True, False)
-                score_pass(whole[h][:], 0, 0, h, False, False)
-                if h == 0:
-                    coarse_pass(0)
-            fine_passes(0)
+            coarse_pass(0)
+            score_pass(whole[0][:], ASIDE, 0, 0, True, False)
+            score_pass(whole[0][:], ASIDE, 0, 0, False, False)
             coarse_pass(1)
-            fine_passes(1)
-            weigh(0, whole[0][:], 0, P // 2)
-            nc.vector.tensor_tensor(summed[:, halves[0]], fine_bank[0][:], coarse[:, halves[0]], ALU.add)
-            weigh(0, whole[1][:], P // 2, P // 2)
-            weigh(SUMMED, summed[:, halves[0]], 0, P // 2)
-            nc.vector.tensor_tensor(summed[:, halves[1]], fine_bank[1][:], coarse[:, halves[1]], ALU.add)
-            weigh(SUMMED, summed[:, halves[1]], P // 2, P // 2)
+            score_pass(whole[1][:], ASIDE, 0, 1, True, False)
+            score_pass(fine_bank[0][:], SUMMED, 1, 0, True, True)
+            score_pass(whole[1][:], ASIDE, 0, 1, False, False)
+            aside_pass(0)
+            score_pass(fine_bank[1][:], SUMMED, 1, 1, True, True)
+            aside_pass(1)
+            for h in range(2):
+                nc.vector.tensor_tensor(summed[:, halves[h]], fine_bank[h][:], coarse[:, halves[h]], ALU.add)
+            for h in range(2):
+                weigh(SUMMED, summed[:, halves[h]], g_held, P // 2 * h, P // 2)
 
         def score(c):
             bank = psum.tile([P, H], F32, name="score", tag=["c", "d"][c - 2])
@@ -228,12 +231,16 @@ def tile_picked_rpqscore_relu_po_kernel(
 
         late = {}
         first_scores()
+        nc.scalar.copy(
+            w_dealt[:].bitcast(U16).rearrange("p (t m) -> p t m", t=4), w_raw[:].bitcast(U16).rearrange("p (m t) -> p t m", t=4)
+        )
+        nc.gpsimd.tensor_copy(w_plane[:].rearrange("p (t m) -> p t m", t=4), ws_raw[:].rearrange("p (m t) -> p t m", t=4))
         for c in range(2, TILES):
             late[c] = score(c)
-        turn(0)
         turn(SUMMED)
+        turn(ASIDE)
         for c in range(2, TILES):
-            weigh(c, late[c][:], 0, P)
+            weigh(c, late[c][:], g_rows[:], 0, P)
             turn(c)
         for stage in (values, planes_out):
             for c in range(TILES):

@@ -22,7 +22,7 @@ TILES = S // P
 LAST = TILES - 1
 HALF = S // 2
 SUMMED = 0
-ASIDE = 1
+ASIDE = 2
 ZERO_SPLIT = 3 * G // 4
 
 
@@ -67,10 +67,10 @@ def tile_picked_rpqscore_relu_po_kernel(
 
         g_scaled = keep.tile([P, 4], F32, name="g_scaled")
         nc.scalar.activation(g_scaled[:], g_raw[:], ACT.Copy, scale=0.03125)
-        g_bank = psum.tile([P, 4, P], F32, name="g_bank", tag="a")
+        g_bank = psum.tile([P, 2, P, 2], F32, name="g_bank", tag="a")
         for t in range(4):
-            nc.tensor.transpose(g_bank[:, t, :], g_scaled[:, t : t + 1].to_broadcast([P, P]), ident[:])
-        nc.scalar.copy(g_rows[:], g_bank[:].rearrange("p (u e) m -> p u m e", e=2))
+            nc.tensor.transpose(g_bank[:, t // 2, :, t % 2], g_scaled[:, t : t + 1].to_broadcast([P, P]), ident[:])
+        nc.scalar.copy(g_rows[:], g_bank[:])
 
         nc.vector.tensor_copy(picked[:, 0:S], xs_table[:].indirect(offs_t[:]))
         nc.vector.tensor_copy(picked[:, S : S + H], ds_table[:].indirect(k1_t[:]))
@@ -123,13 +123,11 @@ def tile_picked_rpqscore_relu_po_kernel(
         y_round = [keep.tile([P, 2 * P, 4], BF16, name=f"y_round{h}", align_bytes=64) for h in range(2)]
         coarse = keep.tile([P, H], F32, name="coarse", align_bytes=64)
         summed = keep.tile([P, H], F32, name="summed", align_bytes=64)
-        turn_tags = ["g", "e", "h", "f"]
-        out_tags = [["b", "a"], ["g"], ["e"], ["c", "h"]]
+        turn_tags = ["e", "h", "b", "f"]
+        out_tags = [["a", "c"], ["e"], ["h"], ["g", "b"]]
         for c in range(TILES):
             z_rows[c] = keep.tile([P, 2, P, 2], BF16, name=f"z_rows{c}", align_bytes=64)
             z_cols[c] = keep.tile([P, P, 4], BF16, name=f"z_cols{c}", align_bytes=64)
-
-        g_held = g_bank[:].rearrange("p (u e) m -> p u m e", e=2)
 
         def weigh(c, scores, weights, first, count):
             view = scores.rearrange("p (m u e) -> p u m e", u=2, e=2)
@@ -167,15 +165,19 @@ def tile_picked_rpqscore_relu_po_kernel(
             for h in range(2):
                 nc.vector.tensor_tensor(summed[:, halves[h]], fine_bank[h][:], coarse[:, halves[h]], ALU.add)
             for h in range(2):
-                weigh(SUMMED, summed[:, halves[h]], g_held, P // 2 * h, P // 2)
+                weigh(SUMMED, summed[:, halves[h]], g_bank[:], P // 2 * h, P // 2)
 
-        def score(c):
-            bank = psum.tile([P, H], F32, name="score", tag=["c", "d"][c - 2])
+        def score(c, tags):
+            width = H // len(tags)
+            parts = [psum.tile([P, width], F32, name="score", tag=tag) for tag in tags]
             for v, again in ((0, 2), (1, 1)):
                 for h in range(2):
+                    first = HALF * h % width
+                    opens = v == 0 and first == 0
+                    closes = v == 1 and first + HALF == width
                     for n in range(again):
-                        score_pass(bank[:, HALF * h : HALF * (h + 1)], c, v, h, (v, h, n) == (0, 0, 0), (v, h) == (1, 1))
-            return bank
+                        score_pass(parts[HALF * h // width][:, first : first + HALF], c, v, h, opens and n == 0, closes)
+            return parts
 
         def turn(c):
             turned = psum.tile([P, 2, P], F32, name="turned", tag=turn_tags[c])
@@ -229,19 +231,20 @@ def tile_picked_rpqscore_relu_po_kernel(
                     out=y_codes[:, cols].bitcast(FP8X4), scales=y_scales[:, cols], in_=y_round[c // 2][:].rearrange("p j t -> p (j t)")
                 )
 
-        late = {}
         first_scores()
         nc.scalar.copy(
             w_dealt[:].bitcast(U16).rearrange("p (t m) -> p t m", t=4), w_raw[:].bitcast(U16).rearrange("p (m t) -> p t m", t=4)
         )
         nc.gpsimd.tensor_copy(w_plane[:].rearrange("p (t m) -> p t m", t=4), ws_raw[:].rearrange("p (m t) -> p t m", t=4))
-        for c in range(2, TILES):
-            late[c] = score(c)
+        second = score(1, ["c"])
+        last = score(LAST, ["d", "g"])
         turn(SUMMED)
+        weigh(1, second[0][:], g_rows[:], 0, P)
+        turn(1)
         turn(ASIDE)
-        for c in range(2, TILES):
-            weigh(c, late[c][:], g_rows[:], 0, P)
-            turn(c)
+        for h in range(2):
+            weigh(LAST, last[h][:], g_rows[:], P // 2 * h, P // 2)
+        turn(LAST)
         for stage in (values, planes_out):
             for c in range(TILES):
                 stage(c)

@@ -22,7 +22,7 @@ TILES = S // P
 LAST = TILES - 1
 HALF = S // 2
 SUMMED = 0
-ASIDE = 2
+ASIDE = 1
 ZERO_SPLIT = 3 * G // 4
 
 
@@ -41,27 +41,25 @@ def tile_picked_rpqscore_relu_po_kernel(
         d_table = keep.tile([P, G], I32, name="d_table", align_bytes=64)
         xs_table = keep.tile([P, T], U8, name="xs_table", align_bytes=64)
         ds_table = keep.tile([P, G], U8, name="ds_table", align_bytes=64)
-        picked = keep.tile([P, S + H], U8, name="picked", align_bytes=64)
-        planes = keep.tile([P, S + H], U8, name="planes", align_bytes=64)
-        picked_d2 = keep.tile([P, H], U8, name="picked_d2", align_bytes=64)
-        d2_plane = keep.tile([P, H], U8, name="d2_plane", align_bytes=64)
+        picked = [keep.tile([P, H + HALF], U8, name=f"picked{v}", align_bytes=64) for v in range(2)]
+        planes = [keep.tile([P, H + HALF], U8, name=f"planes{v}", align_bytes=64) for v in range(2)]
         w_raw = keep.tile([P, 2 * N], U8, name="w_raw", align_bytes=64)
         g_raw = keep.tile([P, 4], F32, name="g_raw")
         g_rows = keep.tile([P, 2, P, 2], F32, name="g_rows", align_bytes=64)
         ident = keep.tile([P, P], F32, name="ident")
 
-        nc.vector.memset(ds_table[:, 0:ZERO_SPLIT].bitcast(I32), 0)
-        nc.gpsimd.memset(ds_table[:, ZERO_SPLIT:G].bitcast(I32), 0)
-        nc.vector.memset(planes[:].bitcast(I32), 0)
-        nc.vector.memset(d2_plane[:].bitcast(I32), 0)
+        nc.vector.memset(xs_table[:, 0:ZERO_SPLIT].bitcast(I32), 0)
+        nc.gpsimd.memset(xs_table[:, ZERO_SPLIT:T].bitcast(I32), 0)
+        for v in range(2):
+            nc.vector.memset(planes[v][:].bitcast(I32), 0)
         make_identity(nc, ident[:])
 
-        nc.sync.dma_start(xs_table[:].bitcast(I32), x_scales[0].bitcast(I32).unsqueeze(1).to_broadcast([16, 8, T // 4]))
-        nc.sync.dma_start(offs_t[:], offs)
-        nc.sync.dma_start(g_raw[:], gn.rearrange("(p t) o -> p (t o)", t=4))
+        nc.sync.dma_start(ds_table[:].bitcast(I32), d_scales[0].bitcast(I32).unsqueeze(1).to_broadcast([16, 8, G // 4]))
         nc.sync.dma_start(k1_t[:], k1)
+        nc.sync.dma_start(g_raw[:], gn.rearrange("(p t) o -> p (t o)", t=4))
+        nc.sync.dma_start(offs_t[:], offs)
+        nc.sync.dma_start(xs_table[0:P:8, :].bitcast(I32), x_scales[0].bitcast(I32))
         nc.sync.dma_start(k2_t[:], k2)
-        nc.sync.dma_start(ds_table[0:P:8, :].bitcast(I32), d_scales[0].bitcast(I32))
         nc.sync.dma_start(x_table[:], x_words[0].rearrange("p n t -> p (n t)").bitcast(I32))
         nc.sync.dma_start(d_table[:], d_words[0].rearrange("p n t -> p (n t)").bitcast(I32))
 
@@ -72,13 +70,13 @@ def tile_picked_rpqscore_relu_po_kernel(
             nc.tensor.transpose(g_bank[:, t // 2, :, t % 2], g_scaled[:, t : t + 1].to_broadcast([P, P]), ident[:])
         nc.scalar.copy(g_rows[:], g_bank[:])
 
-        nc.vector.tensor_copy(picked[:, 0:S], xs_table[:].indirect(offs_t[:]))
-        nc.vector.tensor_copy(picked[:, S : S + H], ds_table[:].indirect(k1_t[:]))
-        nc.vector.tensor_copy(picked_d2[:], ds_table[:].indirect(k2_t[:]))
-        for source, plane in ((picked, planes), (picked_d2, d2_plane)):
+        for v, picks in enumerate((k1_t, k2_t)):
+            nc.vector.tensor_copy(picked[v][:, 0:H], ds_table[:].indirect(picks[:]))
+            nc.vector.tensor_copy(picked[v][:, H : H + HALF], xs_table[:].indirect(offs_t[:, 16 * v : 16 * (v + 1)]))
+        for v in range(2):
             for q in range(4):
-                queue = nc.sync if (plane is d2_plane and q >= 2) else nc.scalar
-                queue.dma_start(plane[32 * q : 32 * q + 4, :].bitcast(I32), source[32 * q : 32 * q + 32 : 8, :].bitcast(I32))
+                queue = nc.sync if (v == 1 and q >= 2) else nc.scalar
+                queue.dma_start(planes[v][32 * q : 32 * q + 4, :].bitcast(I32), picked[v][32 * q : 32 * q + 32 : 8, :].bitcast(I32))
         ws_raw = keep.tile([P, N], U8, name="ws_raw", align_bytes=64)
         for q in range(4):
             rows = w1_scales[0, 4 * q : 4 * q + 4, :].bitcast(I32)
@@ -97,13 +95,13 @@ def tile_picked_rpqscore_relu_po_kernel(
         w_plane = keep.tile([P, N], U8, name="w_plane", align_bytes=64)
 
         def score_pass(out, c, v, h, start, stop):
-            key_plane = [planes[:, S : S + H], d2_plane[:]][v]
+            first = H + P * (c % 2)
             nc.tensor.matmul_mx(
                 out=out,
                 lhsT=xq[:, P * c : P * (c + 1)].bitcast(FP8X4),
-                lhsT_scale=planes[:, P * c : P * (c + 1)],
+                lhsT_scale=planes[c // 2][:, first : first + P],
                 rhs=keys[v][h][:].bitcast(FP8X4),
-                rhs_scale=key_plane[:, HALF * h : HALF * (h + 1)],
+                rhs_scale=planes[v][:, HALF * h : HALF * (h + 1)],
                 start=start,
                 stop=stop,
             )
@@ -235,15 +233,15 @@ def tile_picked_rpqscore_relu_po_kernel(
         nc.scalar.copy(
             w_dealt[:].bitcast(U16).rearrange("p (t m) -> p t m", t=4), w_raw[:].bitcast(U16).rearrange("p (m t) -> p t m", t=4)
         )
-        nc.gpsimd.tensor_copy(w_plane[:].rearrange("p (t m) -> p t m", t=4), ws_raw[:].rearrange("p (m t) -> p t m", t=4))
-        second = score(1, ["c"])
+        third = score(2, ["c"])
         last = score(LAST, ["d", "g"])
         turn(SUMMED)
-        weigh(1, second[0][:], g_rows[:], 0, P)
-        turn(1)
         turn(ASIDE)
+        weigh(2, third[0][:], g_rows[:], 0, P)
+        turn(2)
         for h in range(2):
             weigh(LAST, last[h][:], g_rows[:], P // 2 * h, P // 2)
+        nc.vector.tensor_copy(w_plane[:].rearrange("p (t m) -> p t m", t=4), ws_raw[:].rearrange("p (m t) -> p t m", t=4))
         turn(LAST)
         for stage in (values, planes_out):
             for c in range(TILES):

@@ -32,6 +32,7 @@ def tile_picked_rpqscore_relu_po_kernel(
     nc = tc.nc
     with ExitStack() as ctx:
         keep = ctx.enter_context(tc.tile_pool(name="keep", bufs=1))
+        shared = ctx.enter_context(tc.tile_pool(name="shared", bufs=1))
         psum = ctx.enter_context(tc.psum_pool(name="psum", bufs=1))
 
         offs_t = keep.tile([P, S // 16], U16, name="offs_t")
@@ -43,7 +44,7 @@ def tile_picked_rpqscore_relu_po_kernel(
         ds_table = keep.tile([P, G], U8, name="ds_table", align_bytes=64)
         picked = [keep.tile([P, H + HALF], U8, name=f"picked{v}", align_bytes=64) for v in range(2)]
         planes = [keep.tile([P, H + HALF], U8, name=f"planes{v}", align_bytes=64) for v in range(2)]
-        w_raw = keep.tile([P, 2 * N], U8, name="w_raw", align_bytes=64)
+        w_raw = shared.tile([P, 2 * N], U8, name="w_raw", align_bytes=64, offset=2 * HALF)
         g_raw = keep.tile([P, 4], F32, name="g_raw")
         g_rows = keep.tile([P, 2, P, 2], F32, name="g_rows", align_bytes=64)
         ident = keep.tile([P, P], F32, name="ident")
@@ -60,8 +61,9 @@ def tile_picked_rpqscore_relu_po_kernel(
         nc.sync.dma_start(offs_t[:], offs)
         nc.sync.dma_start(xs_table[0:P:8, :].bitcast(I32), x_scales[0].bitcast(I32))
         nc.sync.dma_start(k2_t[:], k2)
-        nc.sync.dma_start(x_table[:], x_words[0].rearrange("p n t -> p (n t)").bitcast(I32))
         nc.sync.dma_start(d_table[:], d_words[0].rearrange("p n t -> p (n t)").bitcast(I32))
+        nc.sync.dma_start(x_table[:], x_words[0].rearrange("p n t -> p (n t)").bitcast(I32))
+        nc.sync.dma_start(w_raw[:].bitcast(I32), w1_words[0].bitcast(I32))
 
         g_scaled = keep.tile([P, 4], F32, name="g_scaled")
         nc.scalar.activation(g_scaled[:], g_raw[:], ACT.Copy, scale=0.03125)
@@ -75,32 +77,38 @@ def tile_picked_rpqscore_relu_po_kernel(
             nc.vector.tensor_copy(picked[v][:, H : H + HALF], xs_table[:].indirect(offs_t[:, 16 * v : 16 * (v + 1)]))
         for v in range(2):
             for q in range(4):
-                queue = nc.sync if (v == 1 and q >= 2) else nc.scalar
-                queue.dma_start(planes[v][32 * q : 32 * q + 4, :].bitcast(I32), picked[v][32 * q : 32 * q + 32 : 8, :].bitcast(I32))
+                nc.scalar.dma_start(planes[v][32 * q : 32 * q + 4, :].bitcast(I32), picked[v][32 * q : 32 * q + 32 : 8, :].bitcast(I32))
         ws_raw = keep.tile([P, N], U8, name="ws_raw", align_bytes=64)
         for q in range(4):
             rows = w1_scales[0, 4 * q : 4 * q + 4, :].bitcast(I32)
             nc.sync.dma_start(ws_raw[32 * q : 32 * q + 32, :].bitcast(I32), rows.unsqueeze(0).to_broadcast([8, 4, N // 4]))
-            if q == 0:
-                nc.sync.dma_start(w_raw[:].bitcast(I32), w1_words[0].bitcast(I32))
-
-        xq = keep.tile([P, S], U32, name="xq", align_bytes=64)
-        nc.vector.tensor_copy(xq[:], x_table[:].bitcast(U32).indirect(offs_t[:]))
-        keys = [[keep.tile([P, HALF], U32, name=f"keys{v}_{h}", align_bytes=64) for h in range(2)] for v in range(2)]
-        for v, picks in enumerate((k1_t, k2_t)):
-            for h in range(2):
-                nc.vector.tensor_copy(keys[v][h][:], d_table[:].bitcast(U32).indirect(picks[:, 16 * h : 16 * (h + 1)]))
 
         w_dealt = keep.tile([P, 2 * N], U8, name="w_dealt", align_bytes=64)
         w_plane = keep.tile([P, N], U8, name="w_plane", align_bytes=64)
+        nc.scalar.copy(
+            w_dealt[:].bitcast(U16).rearrange("p (t m) -> p t m", t=4), w_raw[:].bitcast(U16).rearrange("p (m t) -> p t m", t=4)
+        )
+
+        coarse_keys = keep.tile([P, H], U32, name="coarse_keys", align_bytes=64)
+        nc.vector.tensor_copy(coarse_keys[:], d_table[:].bitcast(U32).indirect(k1_t[:]))
+        xq = {}
+        for first, count in ((ASIDE, 1), (SUMMED, 1), (2, 2)):
+            piece = keep.tile([P, P * count], U32, name=f"xq{first}", align_bytes=64)
+            nc.vector.tensor_copy(piece[:], x_table[:].bitcast(U32).indirect(offs_t[:, 8 * first : 8 * (first + count)]))
+            for n in range(count):
+                xq[first + n] = piece[:, P * n : P * (n + 1)]
+        fine_keys = [shared.tile([P, HALF], U32, name=f"fine_keys{h}", align_bytes=64, offset=4 * HALF * h) for h in range(2)]
+        for h in range(2):
+            nc.vector.tensor_copy(fine_keys[h][:], d_table[:].bitcast(U32).indirect(k2_t[:, 16 * h : 16 * (h + 1)]))
+        keys = [[coarse_keys[:, 0:HALF], coarse_keys[:, HALF:H]], [fine_keys[0][:], fine_keys[1][:]]]
 
         def score_pass(out, c, v, h, start, stop):
             first = H + P * (c % 2)
             nc.tensor.matmul_mx(
                 out=out,
-                lhsT=xq[:, P * c : P * (c + 1)].bitcast(FP8X4),
+                lhsT=xq[c].bitcast(FP8X4),
                 lhsT_scale=planes[c // 2][:, first : first + P],
-                rhs=keys[v][h][:].bitcast(FP8X4),
+                rhs=keys[v][h].bitcast(FP8X4),
                 rhs_scale=planes[v][:, HALF * h : HALF * (h + 1)],
                 start=start,
                 stop=stop,
@@ -150,9 +158,9 @@ def tile_picked_rpqscore_relu_po_kernel(
                 nc.scalar.activation(kept[:, h], whole[h][:].rearrange("p (m u e) -> p u m e", u=2, e=2), ACT.Relu)
                 nc.gpsimd.tensor_tensor(z_rows[ASIDE][:, :, spans[h]], kept[:, h], g_rows[:, :, spans[h]], ALU.mult)
 
-            coarse_pass(0)
             score_pass(whole[0][:], ASIDE, 0, 0, True, False)
             score_pass(whole[0][:], ASIDE, 0, 0, False, False)
+            coarse_pass(0)
             coarse_pass(1)
             score_pass(whole[1][:], ASIDE, 0, 1, True, False)
             score_pass(fine_bank[0][:], SUMMED, 1, 0, True, True)
@@ -230,18 +238,15 @@ def tile_picked_rpqscore_relu_po_kernel(
                 )
 
         first_scores()
-        nc.scalar.copy(
-            w_dealt[:].bitcast(U16).rearrange("p (t m) -> p t m", t=4), w_raw[:].bitcast(U16).rearrange("p (m t) -> p t m", t=4)
-        )
         third = score(2, ["c"])
         last = score(LAST, ["d", "g"])
         turn(SUMMED)
         turn(ASIDE)
         weigh(2, third[0][:], g_rows[:], 0, P)
+        nc.vector.tensor_copy(w_plane[:].rearrange("p (t m) -> p t m", t=4), ws_raw[:].rearrange("p (m t) -> p t m", t=4))
         turn(2)
         for h in range(2):
             weigh(LAST, last[h][:], g_rows[:], P // 2 * h, P // 2)
-        nc.vector.tensor_copy(w_plane[:].rearrange("p (t m) -> p t m", t=4), ws_raw[:].rearrange("p (m t) -> p t m", t=4))
         turn(LAST)
         for stage in (values, planes_out):
             for c in range(TILES):

from contextlib import ExitStack

import concourse.mybir as mybir
from concourse.masks import make_identity

K, T, S, N, G, H = 512, 2048, 512, 512, 2048, 512
FLOPS = 2 * K * H * S * 2 + 2 * H * N * S

F32 = mybir.dt.float32
BF16 = mybir.dt.bfloat16
I32 = mybir.dt.int32
U32 = mybir.dt.uint32
U16 = mybir.dt.uint16
U8 = mybir.dt.uint8
FP8X4 = mybir.dt.float8_e4m3fn_x4
FP4X4 = mybir.dt.float4_e2m1fn_x4
ALU = mybir.AluOpType
ACT = mybir.ActivationFunctionType

P = 128
TILES = S // P
LAST = TILES - 1
HALF = S // 2
SUMMED = 0
ASIDE = 1
ZERO_SPLIT = 3 * G // 4


def tile_picked_rpqscore_relu_po_kernel(
    tc, x_words, x_scales, d_words, d_scales, gn, w1_words, w1_scales, offs, k1, k2, out_0, out_1, out_2
):
    nc = tc.nc
    with ExitStack() as ctx:
        keep = ctx.enter_context(tc.tile_pool(name="keep", bufs=1))
        shared = ctx.enter_context(tc.tile_pool(name="shared", bufs=1))
        psum = ctx.enter_context(tc.psum_pool(name="psum", bufs=1))

        offs_t = keep.tile([P, S // 16], U16, name="offs_t")
        k1_t = keep.tile([P, H // 16], U16, name="k1_t")
        k2_t = keep.tile([P, H // 16], U16, name="k2_t")
        x_table = keep.tile([P, T], I32, name="x_table", align_bytes=64)
        d_table = keep.tile([P, G], I32, name="d_table", align_bytes=64)
        xs_table = keep.tile([P, T], U8, name="xs_table", align_bytes=64)
        ds_table = keep.tile([P, G], U8, name="ds_table", align_bytes=64)
        picked = [keep.tile([P, H + HALF], U8, name=f"picked{v}", align_bytes=64) for v in range(2)]
        planes = [keep.tile([P, H + HALF], U8, name=f"planes{v}", align_bytes=64) for v in range(2)]
        w_raw = shared.tile([P, 2 * N], U8, name="w_raw", align_bytes=64, offset=2 * HALF)
        g_raw = keep.tile([P, 4], F32, name="g_raw")
        g_rows = keep.tile([P, 2, P, 2], F32, name="g_rows", align_bytes=64)
        ident = keep.tile([P, P], F32, name="ident")

        nc.vector.memset(xs_table[:, 0:ZERO_SPLIT].bitcast(I32), 0)
        nc.gpsimd.memset(xs_table[:, ZERO_SPLIT:T].bitcast(I32), 0)
        for v in range(2):
            nc.vector.memset(planes[v][:].bitcast(I32), 0)
        make_identity(nc, ident[:])

        nc.sync.dma_start(ds_table[:].bitcast(I32), d_scales[0].bitcast(I32).unsqueeze(1).to_broadcast([16, 8, G // 4]))
        nc.sync.dma_start(k1_t[:], k1)
        nc.sync.dma_start(g_raw[:], gn.rearrange("(p t) o -> p (t o)", t=4))
        nc.sync.dma_start(offs_t[:], offs)
        nc.sync.dma_start(xs_table[0:P:8, :].bitcast(I32), x_scales[0].bitcast(I32))
        nc.sync.dma_start(k2_t[:], k2)
        nc.sync.dma_start(d_table[:], d_words[0].rearrange("p n t -> p (n t)").bitcast(I32))
        nc.sync.dma_start(x_table[:], x_words[0].rearrange("p n t -> p (n t)").bitcast(I32))
        nc.sync.dma_start(w_raw[:].bitcast(I32), w1_words[0].bitcast(I32))

        g_scaled = keep.tile([P, 4], F32, name="g_scaled")
        nc.scalar.activation(g_scaled[:], g_raw[:], ACT.Copy, scale=0.03125)
        g_bank = psum.tile([P, 2, P, 2], F32, name="g_bank", tag="a")
        for t in range(4):
            nc.tensor.transpose(g_bank[:, t // 2, :, t % 2], g_scaled[:, t : t + 1].to_broadcast([P, P]), ident[:])
        nc.scalar.copy(g_rows[:], g_bank[:])

        for v, picks in enumerate((k1_t, k2_t)):
            nc.vector.tensor_copy(picked[v][:, 0:H], ds_table[:].indirect(picks[:]))
            nc.vector.tensor_copy(picked[v][:, H : H + HALF], xs_table[:].indirect(offs_t[:, 16 * v : 16 * (v + 1)]))
        for v in range(2):
            for q in range(4):
                nc.scalar.dma_start(planes[v][32 * q : 32 * q + 4, :].bitcast(I32), picked[v][32 * q : 32 * q + 32 : 8, :].bitcast(I32))
        ws_raw = keep.tile([P, N], U8, name="ws_raw", align_bytes=64)
        for q in range(4):
            rows = w1_scales[0, 4 * q : 4 * q + 4, :].bitcast(I32)
            nc.sync.dma_start(ws_raw[32 * q : 32 * q + 32, :].bitcast(I32), rows.unsqueeze(0).to_broadcast([8, 4, N // 4]))

        w_dealt = keep.tile([P, 2 * N], U8, name="w_dealt", align_bytes=64)
        w_plane = keep.tile([P, N], U8, name="w_plane", align_bytes=64)
        nc.scalar.copy(
            w_dealt[:].bitcast(U16).rearrange("p (t m) -> p t m", t=4), w_raw[:].bitcast(U16).rearrange("p (m t) -> p t m", t=4)
        )

        coarse_keys = keep.tile([P, H], U32, name="coarse_keys", align_bytes=64)
        nc.vector.tensor_copy(coarse_keys[:], d_table[:].bitcast(U32).indirect(k1_t[:]))
        xq = {}
        for first, count in ((ASIDE, 1), (SUMMED, 1), (2, 2)):
            piece = keep.tile([P, P * count], U32, name=f"xq{first}", align_bytes=64)
            nc.vector.tensor_copy(piece[:], x_table[:].bitcast(U32).indirect(offs_t[:, 8 * first : 8 * (first + count)]))
            for n in range(count):
                xq[first + n] = piece[:, P * n : P * (n + 1)]
        fine_keys = [shared.tile([P, HALF], U32, name=f"fine_keys{h}", align_bytes=64, offset=4 * HALF * h) for h in range(2)]
        for h in range(2):
            nc.vector.tensor_copy(fine_keys[h][:], d_table[:].bitcast(U32).indirect(k2_t[:, 16 * h : 16 * (h + 1)]))
        keys = [[coarse_keys[:, 0:HALF], coarse_keys[:, HALF:H]], [fine_keys[0][:], fine_keys[1][:]]]

        def score_pass(out, c, v, h, start, stop):
            first = H + P * (c % 2)
            nc.tensor.matmul_mx(
                out=out,
                lhsT=xq[c].bitcast(FP8X4),
                lhsT_scale=planes[c // 2][:, first : first + P],
                rhs=keys[v][h].bitcast(FP8X4),
                rhs_scale=planes[v][:, HALF * h : HALF * (h + 1)],
                start=start,
                stop=stop,
            )

        y_codes = keep.tile([P, S], I32, name="y_codes", align_bytes=64)
        y_scales = keep.tile([P, S], U8, name="y_scales", align_bytes=64)
        out_rows = out_0.rearrange("(p t) j -> p t j", t=4)
        out_words = out_1[0].rearrange("p j t -> p (j t)").bitcast(I32)

        z_rows = {}
        z_cols = {}
        z_codes = [keep.tile([P, P], U32, name=f"z_codes{c}", align_bytes=64) for c in range(TILES)]
        z_scales = [keep.tile([P, P], U8, name=f"z_scales{c}", align_bytes=64) for c in range(TILES)]
        y_late = keep.tile([P, 4, HALF], F32, name="y_late", align_bytes=64)
        y = [keep.tile([P, 4, P], F32, name=f"y{c}", align_bytes=64) for c in range(2)]
        y = y + [y_late[:, :, 0:P], y_late[:, :, P:HALF]]
        y_round = [keep.tile([P, 2 * P, 4], BF16, name=f"y_round{h}", align_bytes=64) for h in range(2)]
        coarse = keep.tile([P, H], F32, name="coarse", align_bytes=64)
        summed = keep.tile([P, H], F32, name="summed", align_bytes=64)
        turn_tags = ["e", "h", "b", "f"]
        out_tags = [["a", "c"], ["e"], ["h"], ["g", "b"]]
        for c in range(TILES):
            z_rows[c] = keep.tile([P, 2, P, 2], BF16, name=f"z_rows{c}", align_bytes=64)
            z_cols[c] = keep.tile([P, P, 4], BF16, name=f"z_cols{c}", align_bytes=64)

        def weigh(c, scores, weights, first, count):
            view = scores.rearrange("p (m u e) -> p u m e", u=2, e=2)
            for u in range(2):
                span = slice(first, first + count)
                nc.vector.scalar_tensor_tensor(z_rows[c][:, u, span], view[:, u], 0.0, weights[:, u, span], ALU.max, ALU.mult)

        def first_scores():
            whole = [psum.tile([P, HALF], F32, name="whole", tag=tag) for tag in ("h", "b")]
            coarse_bank = [psum.tile([P, HALF], F32, name="coarse_bank", tag=tag) for tag in ("c", "d")]
            fine_bank = [psum.tile([P, HALF], F32, name="fine_bank", tag=tag) for tag in ("e", "f")]
            halves = [slice(0, HALF), slice(HALF, H)]
            spans = [slice(0, P // 2), slice(P // 2, P)]
            kept = keep.tile([P, 2, 2, P // 2, 2], F32, name="kept", align_bytes=64)

            def coarse_pass(h):
                score_pass(coarse_bank[h][:], SUMMED, 0, h, True, True)
                nc.scalar.activation(coarse[:, halves[h]], coarse_bank[h][:], ACT.Copy, scale=2.0)

            def aside_pass(h):
                score_pass(whole[h][:], ASIDE, 1, h, False, True)
                nc.scalar.activation(kept[:, h], whole[h][:].rearrange("p (m u e) -> p u m e", u=2, e=2), ACT.Relu)
                nc.gpsimd.tensor_tensor(z_rows[ASIDE][:, :, spans[h]], kept[:, h], g_rows[:, :, spans[h]], ALU.mult)

            score_pass(whole[0][:], ASIDE, 0, 0, True, False)
            score_pass(whole[0][:], ASIDE, 0, 0, False, False)
            coarse_pass(0)
            coarse_pass(1)
            score_pass(whole[1][:], ASIDE, 0, 1, True, False)
            score_pass(fine_bank[0][:], SUMMED, 1, 0, True, True)
            score_pass(whole[1][:], ASIDE, 0, 1, False, False)
            aside_pass(0)
            score_pass(fine_bank[1][:], SUMMED, 1, 1, True, True)
            aside_pass(1)
            for h in range(2):
                nc.vector.tensor_tensor(summed[:, halves[h]], fine_bank[h][:], coarse[:, halves[h]], ALU.add)
            for h in range(2):
                weigh(SUMMED, summed[:, halves[h]], g_bank[:], P // 2 * h, P // 2)

        def score(c, tags):
            width = H // len(tags)
            parts = [psum.tile([P, width], F32, name="score", tag=tag) for tag in tags]
            for v, again in ((0, 2), (1, 1)):
                for h in range(2):
                    first = HALF * h % width
                    opens = v == 0 and first == 0
                    closes = v == 1 and first + HALF == width
                    for n in range(again):
                        score_pass(parts[HALF * h // width][:, first : first + HALF], c, v, h, opens and n == 0, closes)
            return parts

        def turn(c):
            turned = psum.tile([P, 2, P], F32, name="turned", tag=turn_tags[c])
            words = z_rows[c][:].rearrange("p u m e -> p (u m e)").bitcast(F32)
            for u in range(2):
                nc.tensor.transpose(turned[:, u, :], words[:, P * u : P * (u + 1)], ident[:])
            nc.scalar.copy(
                z_cols[c][:].rearrange("p j t -> p (j t)").bitcast(F32).rearrange("p (j u) -> p j u", u=2),
                turned[:].rearrange("p u j -> p j u"),
            )

        def values(c):
            nc.vector.quantize_mx(
                out=z_codes[c][:].bitcast(FP8X4), scales=z_scales[c][:], in_=z_cols[c][:].rearrange("p j t -> p (j t)")
            )
            each = 4 // len(out_tags[c])
            parts = [psum.tile([P, each, P], F32, name="out_bank", tag=tag) for tag in out_tags[c]]
            for t in range(4):
                nc.tensor.matmul_mx(
                    out=parts[t // each][:, t % each, :],
                    lhsT=w_dealt[:, 2 * P * t : 2 * P * (t + 1)].bitcast(FP4X4),
                    lhsT_scale=w_plane[:, P * t : P * (t + 1)],
                    rhs=z_codes[c][:].bitcast(FP8X4),
                    rhs_scale=z_scales[c][:],
                    start=True,
                    stop=True,
                )
            cols = slice(P * c, P * (c + 1))
            if c == 0:
                for h in range(2):
                    nc.scalar.copy(y[c][:, 2 * h : 2 * h + 2], parts[h][:])
                    nc.sync.dma_start(out_rows[:, 2 * h : 2 * h + 2, cols], y[c][:, 2 * h : 2 * h + 2])
                return
            if c == 1:
                nc.vector.tensor_copy(y[c][:], parts[0][:])
            else:
                nc.scalar.copy(y[c][:, 0:each], parts[0][:])
            if each < 4:
                nc.vector.tensor_copy(y[c][:, each:4], parts[1][:])
            if c == 1:
                nc.sync.dma_start(out_rows[:, :, cols], y[c][:])
            if c == LAST:
                nc.sync.dma_start(out_rows[:, :, HALF:S], y_late[:])

        def planes_out(c):
            copy = [nc.gpsimd.tensor_copy, nc.vector.tensor_copy, nc.scalar.copy, nc.vector.tensor_copy][c]
            copy(y_round[c // 2][:, P * (c % 2) : P * (c % 2 + 1)], y[c][:].rearrange("p t j -> p j t"))
            if c % 2 == 1:
                cols = slice(P * (c - 1), P * (c + 1))
                nc.vector.quantize_mx(
                    out=y_codes[:, cols].bitcast(FP8X4), scales=y_scales[:, cols], in_=y_round[c // 2][:].rearrange("p j t -> p (j t)")
                )

        first_scores()
        third = score(2, ["c"])
        last = score(LAST, ["d", "g"])
        turn(SUMMED)
        turn(ASIDE)
        weigh(2, third[0][:], g_rows[:], 0, P)
        nc.vector.tensor_copy(w_plane[:].rearrange("p (t m) -> p t m", t=4), ws_raw[:].rearrange("p (m t) -> p t m", t=4))
        turn(2)
        for h in range(2):
            weigh(LAST, last[h][:], g_rows[:], P // 2 * h, P // 2)
        turn(LAST)
        for stage in (values, planes_out):
            for c in range(TILES):
                stage(c)

        nc.sync.dma_start(out_words, y_codes[:])
        for q in range(4):
            queue = nc.scalar if q % 2 == 0 else nc.sync
            queue.dma_start(out_2[0, 4 * q : 4 * q + 4, :].bitcast(I32), y_scales[32 * q : 32 * q + 4, :].bitcast(I32))
